import numpy as np, ml_dtypes
CORES = [3,11,19,27,35,43]
N = 6
BF = ml_dtypes.bfloat16
def f(rng, *shape):
    return (rng.standard_normal(shape, dtype=np.float32) * np.exp2(rng.integers(-2, 3, shape[:-1] + (1,)))).astype(BF)
def wide(rng, *shape):
    v = f(rng, *shape).astype(np.float32); k = shape[:-2] + (1, shape[-1])
    return (v * np.exp2(rng.integers(-6, 7, k)) * (rng.random(k) > 0.0625)).astype(BF)
P, NT, W, D = 1536, 192, 768, 32
def order(g):
    return range(N) if g < 4 else range(N - 1, -1, -1)
def places(ln):
    n = np.asarray(ln).reshape(-1, NT).astype(np.int64) + 1; m = len(n)
    t = np.repeat(np.tile(np.arange(NT), m), n.reshape(-1)).reshape(m, P)
    last = np.zeros((m, P), bool); last[np.arange(m)[:, None], np.add.accumulate(n, 1) - 1] = True
    return t, last
def steps(ln, ds):
    t, last = places(ln); m = len(t); src = np.arange(P) - np.take_along_axis(np.asarray(ds).reshape(m, NT).astype(np.int64), t, 1)
    e = np.zeros((m, P), np.int64); row = np.arange(m)
    for i in range(P):
        j = src[:, i]; e[:, i] = np.where(last[:, i], 0, 1 + np.where(j >= 0, e[row, np.maximum(j, 0)], 0))
    return e
def lengths(rng, at, big):
    n = np.zeros((N, 8, NT), np.int64)
    for r in range(N):
        for g in range(8):
            b = int(big[r, g]); rest = P - NT - b
            v = np.minimum(rng.multinomial(rest, rng.dirichlet(np.where(rng.random(NT - 1) < 0.25, 0.001, 1.0))), D)
            v = v + rng.multivariate_hypergeometric(D - v, rest - int(np.sum(v)))
            n[r, g] = np.insert(v, int(at[r, g]), b)
    return n
def starts(n):
    return np.add.accumulate(n + 1, 2) - n - 1
def distances(rng, n):
    s = starts(n); k = rng.integers(0, 4, n.shape)
    over = rng.integers(np.minimum(s, W - 1) + 1, W + 1)
    return np.where(k == 0, rng.integers(1, 9, n.shape), np.where(k == 3, over, rng.integers(1, W + 1, n.shape)))
def inside(rng, n, d, share):
    s = starts(n); d = np.array(d)
    for g in range(8):
        q = order(g)[0]; m = (d[q, g] > s[q, g]) & (s[q, g] > 0) & (rng.random(NT) < share)
        d[q, g] = np.where(m, rng.integers(1, np.maximum(s[q, g], 1) + 1), d[q, g])
    return d
def fit(n, d):
    d = np.array(d)
    for r in range(N):
        for g in range(8):
            e = []
            for t, (c, k) in enumerate(zip(n[r, g].tolist(), d[r, g].tolist())):
                s = len(e)
                for i in range(s, s + c): e.append(1 + (e[i - k] if i >= k else 0))
                if max(e[s:], default=0) > D:
                    d[r, g, t] = 1; e[s:] = range(1, c + 1)
                e.append(0)
    return d
def pack(rng, n, d):
    return {"ln": n.astype(np.int32), "ds": d.astype(np.int32), "le": f(rng, N, 128, NT)}
def setup_inputs(rng):
    n = lengths(rng, rng.integers(0, NT, (N, 8)), rng.integers(1, D + 1, (N, 8)))
    return pack(rng, n, fit(n, inside(rng, n, distances(rng, n), 0.75)))
def setup_inputs_deep(rng):
    at = np.where(rng.random((N, 8)) < 0.25, rng.choice(np.array([0, NT - 1]), (N, 8)), rng.integers(0, NT, (N, 8)))
    n = lengths(rng, at, np.full((N, 8), D)); d = np.where(rng.random(n.shape) < 0.5, rng.integers(1, 4, n.shape), distances(rng, n))
    d = inside(rng, n, d, 0.75); np.put_along_axis(d, at[:, :, None], 1, 2)
    return pack(rng, n, fit(n, d))
def setup_inputs_hops(rng):
    n = lengths(rng, rng.integers(0, NT, (N, 8)), rng.integers(1, D + 1, (N, 8)))
    return pack(rng, n, fit(n, inside(rng, n, rng.integers(W - 8, W + 1, n.shape), 1.0)))
def setup_inputs_ends(rng):
    at = rng.choice(np.array([0, NT - 1]), (N, 8)); at[:, :2] = 0
    n = lengths(rng, at, rng.integers(2, D + 1, (N, 8))); n[rng.integers(0, N)] = P // NT - 1
    s = starts(n); d = np.choose(rng.integers(0, 6, n.shape), [s * 0 + W, s * 0 + 1, s, s + 1, s + n, n])
    d = inside(rng, n, np.minimum(np.maximum(d, 1), W), 0.5); d[:, 0, 0] = W; d[:, 1, 0] = 1
    return pack(rng, n, fit(n, d))
def setup_inputs_long(rng):
    at = rng.integers(0, NT, (N, 8)); k = rng.integers(P // D, W + 1, (N, 8)); u = rng.integers(0, 3, (N, 8)); k = np.where(u == 0, P // D, np.where(u == 1, W, k))
    for g in range(8):
        q = order(g)[0]; at[q, g] = NT - 1; k[q, g] = rng.integers(P // D, min(W, NT - 1) + 1)
    n = np.zeros((N, 8, NT), np.int64); np.put_along_axis(n, at[:, :, None], P - NT, 2)
    d = rng.integers(1, W + 1, n.shape); np.put_along_axis(d, at[:, :, None], k[:, :, None], 2)
    return pack(rng, n, d)
def setup_inputs_spread(rng):
    d = setup_inputs(rng); d["le"] = wide(rng, N, 128, NT); return d
def check_inputs(d):
    bad = []; a = np.asarray(d["ln"]).astype(np.int64); b = np.asarray(d["ds"]).astype(np.int64)
    if (a < 0).any() or (np.sum(a, 2) + NT != P).any(): bad.append("lengths")
    if (b < 1).any() or (b > W).any(): bad.append("distances")
    if not bad and (steps(a, b) > D).any(): bad.append("steps")
    if not np.isfinite(np.asarray(d["le"]).astype(np.float32)).all(): bad.append("finite")
    return bad
def reference(ln, ds, le):
    y = np.zeros((N, 128, P), BF); t, last = places(ln); t = t.reshape(N, 8, P); last = last.reshape(N, 8, P)
    for g in range(8):
        buf = np.zeros((W + P, 16), BF)
        for r in order(g):
            a = np.ascontiguousarray(le[r, 16 * g:16 * g + 16].T); k = ds[r, g][t[r, g]].tolist(); tk = t[r, g].tolist(); own = last[r, g].tolist()
            for i in range(P):
                buf[W + i] = a[tk[i]] if own[i] else buf[W + i - k[i]]
            y[r, 16 * g:16 * g + 16] = buf[W:].T
            buf[:W] = buf[P:]
    return {"y": y}

@@ -1,0 +1,291 @@
+from concourse.bass import DstId, RemoteDMATransfer
+from concourse.mybir import AluOpType, ActivationFunctionType
+
+N, P, NT, W = 6, 1536, 192, 768
+H = NT + W
+C = NT // 16
+LW = W // 16
+B = P // 3
+K = 256
+CT, LT, TT, IA, IB = 0, 4, 7, 8, 9
+SCRATCH = {
+    "lnb": ("sbuf", [128, C], "int32"), "dsr": ("sbuf", [128, NT], "int32"),
+    "sc": ("sbuf", [128, C], "float32"), "sch": ("sbuf", [128, 1], "float16"),
+    "lasts": ("sbuf", [128, C], "uint16"), "ci": ("sbuf", [128, C + 1], "int32"), "cl": ("sbuf", [128, C + 2], "uint16"),
+    "pi": ("sbuf", [128, 1], "int32"), "pj": ("sbuf", [128, 1], "int32"), "pf": ("sbuf", [128, 1], "float32"),
+    "cut": ("sbuf", [128, 1], "float32"), "p12": ("sbuf", [128, 1], "float32"), "pm": ("sbuf", [128, 1], "float32"),
+    "mc": ("sbuf", [128, 1], "float32"), "mt": ("sbuf", [128, 1], "float32"),
+    "ma": ("sbuf", [128, 1], "float32"), "mb": ("sbuf", [128, 1], "float32"),
+    "ck": ("sbuf", [128, 10], "float32"), "cb": ("sbuf", [128, 10], "float32"),
+    "ones": ("sbuf", [128, K], "bfloat16"), "cnt": ("sbuf", [128, K], "bfloat16"),
+    "e0": ("sbuf", [128, 132], "float16"), "e1": ("sbuf", [128, 132], "float16"),
+    "qp": ("sbuf", [128, 132], "float16"), "qn": ("sbuf", [128, 132], "float16"),
+    "gt": ("sbuf", [128, 128], "float16"), "tri": ("sbuf", [128, 128], "float16"),
+    "f0": ("sbuf", [128, 144], "bfloat16"), "f1": ("sbuf", [128, 144], "bfloat16"), "f": ("sbuf", [128, 144], "bfloat16"),
+    "lt": ("sbuf", [128, NT], "bfloat16"), "ct": ("sbuf", [128, NT], "bfloat16"),
+    "rd": ("sbuf", [128, NT + 16], "float16"), "z": ("sbuf", [128, NT], "bfloat16"),
+    "d0": ("sbuf", [128, B], "bfloat16"), "d1": ("sbuf", [128, P], "bfloat16"),
+    "wa": ("sbuf", [128, H + P], "bfloat16"), "wb": ("sbuf", [128, H + P], "bfloat16"),
+    "la": ("sbuf", [128, P // 16], "uint16"), "lb": ("sbuf", [128, P // 16], "uint16"), "ol": ("sbuf", [128, P // 16], "uint16"),
+    "idi": ("sbuf", [128, LW], "int32"), "idl": ("sbuf", [128, LW], "uint16"),
+    "ll": ("sbuf", [128, N * LW], "uint16"), "cl5": ("sbuf", [128, N * LW], "uint16"),
+    "yo": ("sbuf", [128, P], "bfloat16"), "ye": ("sbuf", [128, P], "bfloat16"),
+    "dle": ("dram", [2, 128, NT // 2], "bfloat16"), "lel": ("dram", [N, 128, NT // 2], "bfloat16"),
+    "car": ("psum", [128, 512], "float32"), "zp": ("psum", [128, 512], "float32"), "ini": ("psum", [128, 512], "float32"),
+    "cva": ("psum", [128, 512], "float32"), "cvb": ("psum", [128, 512], "float32"),
+}
+for _k in range(N):
+    SCRATCH["sw%d" % _k] = ("sbuf", [128, H], "bfloat16")
+SEMAPHORES = ["cg", "cv", "cs", "cp", "dl", "dd", "dle", "lo", "lw", "lz", "st", "ls"]
+SEMAPHORES += ["ar%d" % k for k in range(N)] + ["la%d" % k for k in range(N)]
+
+
+def rank_program(g, core, T, topo):
+    rank = T.rank_of(core)
+    if rank is None:
+        return
+    A, CP, ID = AluOpType, ActivationFunctionType.Copy, ActivationFunctionType.Identity
+    v, s, pe, sync, S = g.vector, g.scalar, g.tensor, g.sync, T.sem
+    queue = {"g": g, "v": v, "s": s, "p": pe, "y": sync}
+    cnt = {"g": 0, "v": 0, "s": 0, "p": 0}
+    seen = {}
+
+    def need(q, *deps):
+        for sem, val in deps:
+            if seen.get((q, sem), 0) < val:
+                queue[q].wait_ge(S[sem], val)
+                seen[(q, sem)] = val
+
+    def op(q, deps, ins):
+        need(q, *deps)
+        cnt[q] += 1
+        ins().then_inc(S["c" + q], 1)
+        return ("c" + q, cnt[q])
+
+    def ts(out, in0, s1, s2, *ops):
+        return lambda: v.tensor_scalar(out, in0, s1, s2, *ops)
+
+    up, down = rank, N - 1 - rank
+    n = max(up, down)
+    mixed = up > 0 and down > 0
+    others = [r for r in range(N) if r != rank]
+    others.sort(key=lambda r: -abs(r - rank))
+    stage = [(k - (n - up), k - (n - down)) for k in range(n)]
+    stage = [(a if a >= 0 else None, N - 1 - b if b >= 0 else None) for a, b in stage]
+    own = None if mixed else stage[0].index(None)
+    sw = [T["sw%d" % k] for k in range(n + 1)]
+
+    def half(side):
+        return slice(64 * side, 64 * side + 64)
+
+    sync.dma_start(T.lnb[:], T.ln[:]).then_inc(S.dl, 16)
+    dz = op("v", [], lambda: v.memset(T.dsr[:], 0))
+    need("y", dz)
+    need("s", dz)
+    sync.dma_start(T.dsr[CT:128:16, :], T.ds[:]).then_inc(S.dd, 16)
+    s.dma_start(T.dsr[CT + 1:128:16, :], T.ds[:]).then_inc(S.dd, 16)
+    sync.dma_start(T.dsr[CT + 2:128:16, :], T.ds[:]).then_inc(S.dd, 16)
+    sync.dma_start(T.dle[:], T.le[:]).then_inc(S.dle, 16)
+    sync.dma_start(sw[n][:, 0:NT], T.le[:]).then_inc(S.lo, 16)
+    if not mixed:
+        sync.dma_start(sw[0][half(own), 0:NT], T.le[half(own), :]).then_inc(S.lo, 16)
+
+    flag = {"allow_small_or_imprecise_dtypes": True}
+    pi = op("g", [], lambda: g.iota(T.pi[:], [[1, 1]], 0, 1))
+    ci = op("g", [], lambda: g.iota(T.ci[:], [[1, C + 1]], 0, 0))
+    pf = op("g", [], lambda: g.iota(T.pf[:], [[1, 1]], 0, 1, **flag))
+    ck = op("g", [], lambda: g.iota(T.ck[:], [[K, 10]], 0, 0, **flag))
+    lt = op("g", [], lambda: g.iota(T.lt[:], [[1, C], [C, 16]], 0, 0, **flag))
+    ones = op("v", [], lambda: v.memset(T.ones[:], 1.0))
+    pj = op("v", [pi], ts(T.pj[:], T.pi[:], 15, None, A.bitwise_and))
+    co = op("v", [ones], lambda: v.tensor_tensor_scan(T.cnt[:], T.ones[:], T.ones[:], -1.0, A.add, A.mult))
+    mc = op("v", [pj], ts(T.mc[:], T.pj[:], float(CT + 3), None, A.is_lt))
+    p12 = op("v", [], ts(T.p12[:], T.pj[:], float(C), None, A.mult))
+    cut = op("v", [], ts(T.cut[:], T.pj[:], -float(K), None, A.mult))
+    gt = op("v", [co, pf], ts(T.gt[:], T.cnt[:, 0:128], T.pf[:], None, A.is_gt))
+    cl = op("v", [p12, ci], ts(T.cl[:, 0:C + 1], T.ci[:], T.p12[:], float(NT - 1), A.add, A.min))
+    op("v", [], ts(T.e0[:], T.cnt[:, 0:132], T.pf[:], float(LT), A.subtract, A.is_equal))
+    e1 = op("v", [], ts(T.e1[:], T.cnt[:, 0:132], T.pf[:], float(LT - 1), A.subtract, A.is_equal))
+    ma = op("v", [], ts(T.ma[:], T.pj[:], float(IA), None, A.is_equal))
+    mb = op("v", [], ts(T.mb[:], T.pj[:], float(IB), None, A.is_equal))
+    qp = op("v", [e1], lambda: v.tensor_tensor(T.qp[:], T.e0[:], T.e1[:], A.subtract))
+    cb = op("v", [mb, ck], ts(T.cb[:], T.ck[:], T.mb[:], None, A.mult))
+    qn = op("v", [qp], ts(T.qn[:], T.qp[:], -1.0, None, A.mult))
+    mt = op("v", [], ts(T.mt[:], T.pj[:], float(TT), None, A.is_equal))
+    tri = op("g", [gt], lambda: g.affine_select(T.tri[:], T.gt[:], [[-16, 8], [0, 16]], A.is_ge, 0.0, 0, 1))
+    f0 = op("g", [ones], lambda: g.affine_select(T.f0[:], T.ones[:, 0:144], [[-16, 9], [-4096, 16]], A.is_ge, 0.0, 16, 1))
+    f1 = op("g", [f0], lambda: g.affine_select(T.f1[:], T.f0[:], [[16, 9], [-4096, 16]], A.is_ge, 0.0, 14 - 16, -1))
+    f = op("g", [f1], lambda: g.affine_select(T.f[:], T.f1[:], [[-16, 9], [0, 16]], A.not_equal, 0.0, 16 - (CT + 3), 1))
+    idi = op("g", [], lambda: g.iota(T.idi[:], [[16, LW]], NT, 0)) if mixed else None
+
+    def columns(q, deps, out, o, a, b):
+        while a < b:
+            k, e = a // K, min(b, (a // K + 1) * K)
+            src = T.cnt[:, a - K * k:e - K * k]
+            if q == "v":
+                t = op(q, deps, ts(out[:, o:o + e - a], src, T.ma[:], T.cb[:, k:k + 1], A.mult, A.add))
+            else:
+                t = op(q, deps, lambda: s.activation(out[:, o:o + e - a], src, ID, T.cb[:, k:k + 1], T.ma[:]))
+            o, a = o + e - a, e
+        return t
+
+    dc = [op("s", [mc, ones], lambda: s.activation(T.d0[:, x:x + K], T.ones[:], CP, scale=T.mc[:])) for x in (0, K)][-1]
+    x1 = columns("s", [co, ma, cb], T.d1, 1280 - H, 1280, 2048)
+    sc = op("v", [("dl", 16), ones], lambda: v.tensor_tensor_scan(T.sc[:], T.lnb[:], T.ones[:, 0:C], 0.0, A.add, A.add))
+    rd = op("v", [cl, cut, ("dd", 48)], ts(T.rd[:], T.dsr[:, 0:NT].indirect(T.cl[:, 0:C + 1]), T.cut[:], 0.0, A.add, A.max))
+    sch = op("v", [sc], lambda: v.tensor_copy(T.sch[:], T.sc[:, C - 1:C]))
+    car = op("p", [tri, sch], lambda: pe.matmul(T.car[:, 0:1], T.tri[:], T.sch[:], True, True))
+    ct = op("v", [lt, mt], ts(T.ct[:], T.lt[:], T.mt[:], None, A.mult))
+    columns("v", [cb], T.d1, 0, H, 1280)
+    lasts = op("v", [car, sc], ts(T.lasts[:], T.sc[:], T.car[:, 0:1], -1.0, A.add, A.add))
+    x0 = columns("v", [], T.d1, 2048 - H, 2048, H + P)
+    op("p", [qn, rd], lambda: pe.matmul(T.zp[:, 0:NT], T.qn[:, LT:LT + 128], T.rd[:, 16:NT + 16], True, False))
+    op("p", [], lambda: pe.matmul(T.zp[:, 0:NT], T.qp[:, LT:LT + 128], T.rd[:, 0:NT], False, False))
+    zp = op("p", [], lambda: pe.matmul(T.zp[:, 0:NT], T.qp[:, 0:128], T.rd[:, 16:NT + 16], False, True))
+    ini = op("p", [], lambda: pe.matmul(T.ini[:, 0:1], T.qn[:, LT:LT + 128], T.rd[:, 0:1], True, True))
+    z = op("v", [zp, ct], lambda: v.tensor_tensor(T.z[:], T.zp[:, 0:NT], T.ct[:], A.add))
+    zs = op("v", [z, lasts, x0, x1], lambda: v.tensor_copy(T.d1[:, 0:P].indirect(T.lasts[:, 0:C]), T.z[:]))
+    r = []
+    for a in range(0, P, B):
+        r.append(op("v", r[-1:] if r else [zs, dc, ini], lambda: v.tensor_tensor_scan(
+            T.wa[:, H + a:H + a + B], T.d0[:], T.d1[:, a:a + B], T.wa[:, H + a - 1:H + a] if a else T.ini[:, 0:1], A.mult, A.add)))
+    ia = [columns("v", [], T.wa, 0, 0, 2 * K), columns("s", [], T.wa, 2 * K, 2 * K, H)]
+    ib = columns("s", [], T.wb, 0, 0, H)
+
+    def ids(rs):
+        out = []
+        for r in rs:
+            a = topo.addr(T.cores[r])
+            out.append(DstId(rid=a[0], pnc=a[1]))
+        return out
+
+    def bits(engines):
+        return sum(1 << e for e in engines)
+
+    def shared(src):
+        es = [topo.engines(T.cores[src], T.cores[r]) for r in range(N) if r != src]
+        return [e for e in es[0] if all(e in x for x in es)]
+
+    def letter_engines(src):
+        e = shared(src)
+        if src == 0:
+            return e, []
+        if src == N - 1:
+            return [], e
+        return e[:len(e) // 2], e[len(e) // 2:]
+
+    trs = []
+    for side, rs in ((0, [r for r in others if r > rank]), (1, [r for r in others if r < rank])):
+        if rs:
+            trs.append(RemoteDMATransfer(dst_ids=ids(rs), dma_engine_mask=bits(letter_engines(rank)[side]), remote_sem=S["la%d" % rank],
+                                         srcs=[T.dle[side]], dsts=[T.lel[rank] for _ in rs]))
+    g.wait_ge(S.dle, 16)
+    g.remote_dma_fused(trs, local_sem=S.ls)
+    sent = sum(len(e) for e in letter_engines(rank))
+
+    blank = [(k, side) for k in range(n) for side in range(2) if stage[k][side] is None]
+    zero = blank if mixed else blank[1:]
+    need("y", op("v", [], lambda: v.memset(T.yo[:, 0:W], 0.0)))
+    sync.dma_start(sw[0][:, NT:H], T.yo[:, 0:W]).then_inc(S.lz, 16)
+    for k, side in zero:
+        sync.dma_start(sw[k][half(side), 0:NT], T.yo[half(side), 0:NT]).then_inc(S.lz, 16)
+    z0 = ("lz", 16 + 16 * len(zero) + (16 * len(blank) if mixed else 0))
+    if mixed:
+        pm = op("v", [], lambda: v.tensor_copy(T.pm[:], T.pj[:]))
+        need("y", op("v", [idi, pm], ts(T.idl[:], T.idi[:], T.pm[:], None, A.add)))
+        for k, side in blank:
+            sync.dma_start(T.cl5[half(side), LW * k:LW * k + LW], T.idl[half(side), :]).then_inc(S.lz, 16)
+
+    def conv(deps, out, win, a, b):
+        need("p", *deps)
+        for q in range(16):
+            t = op("p", [], lambda: pe.matmul(out[:, a // 16:b // 16], T.f[:, 16 - q:144 - q], win[:, H + a + q:H + b:16], q == 0, q == 15))
+        return t
+
+    def emit(dep, out, a, b, src):
+        return op("v", [dep], lambda: v.tensor_copy(out[:, a:b], src[:, a:b]))
+
+    def jump(deps, out, o, win, lst, a, b):
+        h = (a + b) // 2
+        e = o + 16 * (h - a)
+        z = win.shape[1]
+        t1 = op("v", deps, lambda: v.tensor_copy(out[:, o:e], win[:, 0:z].indirect(lst[:, a:h])))
+        t2 = op("s", deps, lambda: s.activation(out[:, e:o + 16 * (b - a)], win[:, 0:z].indirect(lst[:, h:b]), CP))
+        return [t1, t2]
+
+    full, BC = P // 16, B // 16
+    win, oth, lst, nxt = T.wa, T.wb, T.la, T.lb
+    c1, c2 = conv([r[0], f], T.cva, win, 0, B), conv(r[-1:], T.cvb, win, B, P)
+    ready = r[-1:] + ia
+    cols = ((0, BC), (BC, full))
+    later = ((LW, full), (0, LW))
+    for i, (a, b) in enumerate((cols, later, later, later)):
+        e1 = emit(c1, lst, cols[0][0], cols[0][1], T.cva)
+        t1 = jump(ready + [e1], oth, H + 16 * a[0], win, lst, a[0], a[1]) if i != 1 else None
+        e2 = emit(c2, lst, cols[1][0], cols[1][1], T.cvb)
+        if t1 is None:
+            t1 = jump(ready + [e1, e2], oth, H + 16 * a[0], win, lst, a[0], a[1])
+        c1 = conv(t1, T.cva, oth, 16 * a[0], 16 * a[1])
+        t2 = jump([e2], oth, H + 16 * b[0], win, lst, b[0], b[1])
+        c2 = conv(t2, T.cvb, oth, 16 * b[0], 16 * b[1])
+        ready = t1 + t2
+        win, oth = oth, win
+        if i == 0:
+            ready = jump(ready + [ib], oth, H, win, lst, 0, full)
+            win, oth = oth, win
+        lst, nxt = nxt, lst
+        cols = (a, b)
+    e1 = emit(c1, lst, cols[0][0], cols[0][1], T.cva)
+    t = jump(ready + [e1], oth, H + W, win, lst, LW, full)
+    cp = conv(t, T.cva, oth, W, P)
+    e2 = emit(c2, lst, cols[1][0], cols[1][1], T.cvb)
+    t = jump([e2], oth, H, win, lst, 0, LW)
+    cq = conv(t, T.cvb, oth, 0, W)
+    tail = emit(cp, T.ol, LW, full, T.cva)
+    te = []
+    if not mixed:
+        te += jump([tail, z0, ("lo", 32), ("lw", 16 * (up + down))], T.ye, W, sw[0], T.ol, LW, full)
+    head = emit(cq, T.ol, 0, LW, T.cvb)
+    if not mixed:
+        te += jump([head], T.ye, 0, sw[0], T.ol, 0, LW)
+
+    need("g", tail)
+    g.remote_dma_fused([RemoteDMATransfer(dst_ids=ids(others), dma_engine_mask=bits(shared(rank)), remote_sem=S["ar%d" % rank],
+                                          srcs=[T.ol[:, LW:full]], dsts=[T.ll[:, LW * rank:LW * rank + LW] for _ in others])], local_sem=S.ls)
+    sent += len(shared(rank))
+
+    for k in range(n):
+        for side in range(2):
+            src = stage[k][side]
+            if src is not None:
+                need("y", ("la%d" % src, len(letter_engines(src)[side])))
+                sync.dma_start(sw[k][half(side), 0:NT], T.lel[src]).then_inc(S.lw, 16)
+    stored = 0
+    if not mixed:
+        need("y", *te)
+        sync.dma_start(T.y[half(own), :], T.ye[half(own), :]).then_inc(S.st, 16)
+        stored += 16
+
+    ready = [z0, ("lw", 16 * (up + down))]
+    for k in range(n):
+        if mixed:
+            for side in range(2):
+                src = stage[k][side]
+                if src is not None:
+                    ready.append(op("v", [("ar%d" % src, len(shared(src)))], lambda: v.tensor_copy(
+                        T.cl5[half(side), LW * k:LW * k + LW], T.ll[half(side), LW * src:LW * src + LW])))
+            lst, a = T.cl5, LW * k
+        else:
+            src = stage[k][1 - own]
+            ready.append(("ar%d" % src, len(shared(src))))
+            lst, a = T.ll, LW * src
+        ready = jump(ready, sw[k + 1], NT, sw[k], lst, a, a + LW)
+    ready += [head, ("lo", 16 if mixed else 32)]
+    rows = slice(0, 128) if mixed else half(1 - own)
+    for a, b in ((0, 32), (32, 64), (64, 96)):
+        t = jump(ready, T.yo, 16 * a, sw[n], T.ol, a, b)
+        need("y", *t)
+        sync.dma_start(T.y[rows, 16 * a:16 * b], T.yo[rows, 16 * a:16 * b]).then_inc(S.st, 16)
+        stored += 16
+    g.wait_ge(S.ls, sent)
+    need("y", ("st", stored), *[("c" + q, cnt[q]) for q in cnt])

@@ -7,44 +7,67 @@ C = NT // 16
 LW = W // 16
 B = P // 3
 K = 256
-CT, LT, TT, IA, IB = 0, 4, 7, 8, 9
+CT, LT, IA, IB = 0, 4, 8, 9
+VC = 22
+PLAN = [(0, 1), (1, 0), (1, 1), (0, 0), (0, 1), (1, 0), (1, 1), (0, 1), (1, 1), (0, 0)]
+LAG, LAST = {5: 0, 4: 2, 3: 1}, {5: 0.6, 4: 0.4, 3: 1.0}
 SCRATCH = {
     "lnb": ("sbuf", [128, C], "int32"), "dsr": ("sbuf", [128, NT], "int32"),
-    "sc": ("sbuf", [128, C], "float32"), "sch": ("sbuf", [128, 1], "float16"),
+    "sc": ("sbuf", [128, C], "float16"),
     "lasts": ("sbuf", [128, C], "uint16"), "ci": ("sbuf", [128, C + 1], "int32"), "cl": ("sbuf", [128, C + 2], "uint16"),
-    "pi": ("sbuf", [128, 1], "int32"), "pj": ("sbuf", [128, 1], "int32"), "pf": ("sbuf", [128, 1], "float32"),
-    "cut": ("sbuf", [128, 1], "float32"), "p12": ("sbuf", [128, 1], "float32"), "pm": ("sbuf", [128, 1], "float32"),
-    "mc": ("sbuf", [128, 1], "float32"), "mt": ("sbuf", [128, 1], "float32"),
+    "pi": ("sbuf", [128, 1], "int32"), "pj": ("sbuf", [128, 1], "int32"), "xd": ("sbuf", [128, 132], "bfloat16"),
+    "cut": ("sbuf", [128, 1], "float32"), "p12": ("sbuf", [128, 1], "float32"), "mc": ("sbuf", [128, 1], "float32"),
     "ma": ("sbuf", [128, 1], "float32"), "mb": ("sbuf", [128, 1], "float32"),
-    "ck": ("sbuf", [128, 10], "float32"), "cb": ("sbuf", [128, 10], "float32"),
-    "ones": ("sbuf", [128, K], "bfloat16"), "cnt": ("sbuf", [128, K], "bfloat16"),
-    "e0": ("sbuf", [128, 132], "float16"), "e1": ("sbuf", [128, 132], "float16"),
-    "qp": ("sbuf", [128, 132], "float16"), "qn": ("sbuf", [128, 132], "float16"),
-    "gt": ("sbuf", [128, 128], "float16"), "tri": ("sbuf", [128, 128], "float16"),
-    "f0": ("sbuf", [128, 144], "bfloat16"), "f1": ("sbuf", [128, 144], "bfloat16"), "f": ("sbuf", [128, 144], "bfloat16"),
+    "pg": ("sbuf", [128, 1], "int32"), "off": ("sbuf", [128, 1], "float32"),
+    "ck": ("sbuf", [128, 5], "float32"), "cb": ("sbuf", [128, 5], "float32"),
+    "ones": ("sbuf", [128, B], "bfloat16"), "cnt": ("sbuf", [128, B], "bfloat16"),
+    "e0": ("sbuf", [128, 132], "float16"), "qp": ("sbuf", [128, 132], "float16"), "qn": ("sbuf", [128, 128], "float16"),
+    "gt": ("sbuf", [128, 128], "float16"),
+    "f": ("sbuf", [128, 144], "bfloat16"), "f2": ("sbuf", [128, 144], "bfloat16"),
     "lt": ("sbuf", [128, NT], "bfloat16"), "ct": ("sbuf", [128, NT], "bfloat16"),
     "rd": ("sbuf", [128, NT + 16], "float16"), "z": ("sbuf", [128, NT], "bfloat16"),
-    "d0": ("sbuf", [128, B], "bfloat16"), "d1": ("sbuf", [128, P], "bfloat16"),
+    "d0": ("sbuf", [128, W], "bfloat16"), "d1": ("sbuf", [128, P], "bfloat16"),
     "wa": ("sbuf", [128, H + P], "bfloat16"), "wb": ("sbuf", [128, H + P], "bfloat16"),
-    "la": ("sbuf", [128, P // 16], "uint16"), "lb": ("sbuf", [128, P // 16], "uint16"), "ol": ("sbuf", [128, P // 16], "uint16"),
-    "idi": ("sbuf", [128, LW], "int32"), "idl": ("sbuf", [128, LW], "uint16"),
-    "ll": ("sbuf", [128, N * LW], "uint16"), "cl5": ("sbuf", [128, N * LW], "uint16"),
-    "yo": ("sbuf", [128, P], "bfloat16"), "ye": ("sbuf", [128, P], "bfloat16"),
+    "la": ("sbuf", [128, P // 16], "uint16"),
+    "so": ("sbuf", [128, 2 * LW], "uint16"), "ol": ("sbuf", [128, 2 * LW], "uint16"), "ll": ("sbuf", [128, N * LW], "uint16"),
+    "sw": ("sbuf", [128, N * H], "bfloat16"), "se": ("sbuf", [128, H], "bfloat16"),
+    "yo": ("sbuf", [128, P], "bfloat16"),
     "dle": ("dram", [2, 128, NT // 2], "bfloat16"), "lel": ("dram", [N, 128, NT // 2], "bfloat16"),
     "car": ("psum", [128, 512], "float32"), "zp": ("psum", [128, 512], "float32"), "ini": ("psum", [128, 512], "float32"),
-    "cva": ("psum", [128, 512], "float32"), "cvb": ("psum", [128, 512], "float32"),
+    "cva": ("psum", [128, 512], "float32"), "cvb": ("psum", [128, 512], "float32"), "cvc": ("psum", [128, 512], "float32"),
 }
-for _k in range(N):
-    SCRATCH["sw%d" % _k] = ("sbuf", [128, H], "bfloat16")
-SEMAPHORES = ["cg", "cv", "cs", "cp", "dl", "dd", "dle", "lo", "lw", "lz", "st", "ls"]
+SEMAPHORES = ["cg", "cv", "cs", "cp", "dl", "dd", "dle", "lo", "lw", "df", "st", "ls"]
 SEMAPHORES += ["ar%d" % k for k in range(N)] + ["la%d" % k for k in range(N)]
+
+
+def piece(r, side):
+    return N - 1 - r if side else r
+
+
+def long_side(r):
+    return 0 if piece(r, 0) > piece(r, 1) else 1
+
+
+def lag(r):
+    return LAG[piece(r, long_side(r))]
+
+
+def call_of(src, dst):
+    side = 0 if src < dst else 1
+    return piece(src, side) + (lag(dst) if side != long_side(dst) else 0)
+
+
+def gathers_left(src, dst):
+    n = piece(dst, long_side(dst))
+    return n + (1 if n == N - 1 else 2) - call_of(src, dst) + LAST[n]
 
 
 def rank_program(g, core, T, topo):
     rank = T.rank_of(core)
     if rank is None:
         return
-    A, CP, ID = AluOpType, ActivationFunctionType.Copy, ActivationFunctionType.Identity
+    A, F = AluOpType, ActivationFunctionType
+    CP, ID = F.Copy, F.Identity
     v, s, pe, sync, S = g.vector, g.scalar, g.tensor, g.sync, T.sem
     queue = {"g": g, "v": v, "s": s, "p": pe, "y": sync}
     cnt = {"g": 0, "v": 0, "s": 0, "p": 0}
@@ -65,18 +88,22 @@ def rank_program(g, core, T, topo):
     def ts(out, in0, s1, s2, *ops):
         return lambda: v.tensor_scalar(out, in0, s1, s2, *ops)
 
-    up, down = rank, N - 1 - rank
-    n = max(up, down)
-    mixed = up > 0 and down > 0
-    others = [r for r in range(N) if r != rank]
-    others.sort(key=lambda r: -abs(r - rank))
-    stage = [(k - (n - up), k - (n - down)) for k in range(n)]
-    stage = [(a if a >= 0 else None, N - 1 - b if b >= 0 else None) for a, b in stage]
-    own = None if mixed else stage[0].index(None)
-    sw = [T["sw%d" % k] for k in range(n + 1)]
-
     def half(side):
         return slice(64 * side, 64 * side + 64)
+
+    lg = long_side(rank)
+    sh = 1 - lg
+    n, m = piece(rank, lg), piece(rank, sh)
+    end = m == 0
+    lagged = lag(rank)
+    spare = n - m - lagged
+    source = {(side, k): piece(k, side) for side in range(2) for k in range(piece(rank, side))}
+
+    def slot(side, k):
+        return k + lagged if side == sh and k > 0 else k
+
+    def letters(side, k):
+        return T.sw[half(side), H * k:H * k + NT]
 
     sync.dma_start(T.lnb[:], T.ln[:]).then_inc(S.dl, 16)
     dz = op("v", [], lambda: v.memset(T.dsr[:], 0))
@@ -86,71 +113,64 @@ def rank_program(g, core, T, topo):
     s.dma_start(T.dsr[CT + 1:128:16, :], T.ds[:]).then_inc(S.dd, 16)
     sync.dma_start(T.dsr[CT + 2:128:16, :], T.ds[:]).then_inc(S.dd, 16)
     sync.dma_start(T.dle[:], T.le[:]).then_inc(S.dle, 16)
-    sync.dma_start(sw[n][:, 0:NT], T.le[:]).then_inc(S.lo, 16)
-    if not mixed:
-        sync.dma_start(sw[0][half(own), 0:NT], T.le[half(own), :]).then_inc(S.lo, 16)
+    if end:
+        own = [(letters(x, n), lg) for x in range(2)] + [(T.se[half(x), 0:NT], sh) for x in range(2)]
+    else:
+        own = [(letters(x, slot(x, piece(rank, x))), x) for x in range(2)]
 
     flag = {"allow_small_or_imprecise_dtypes": True}
     pi = op("g", [], lambda: g.iota(T.pi[:], [[1, 1]], 0, 1))
+    xd = op("g", [], lambda: g.iota(T.xd[:], [[1, 132]], 0, -1, **flag))
+    ck = op("g", [], lambda: g.iota(T.ck[:], [[B, 5]], H - 2 * B + K, 0, **flag))
     ci = op("g", [], lambda: g.iota(T.ci[:], [[1, C + 1]], 0, 0))
-    pf = op("g", [], lambda: g.iota(T.pf[:], [[1, 1]], 0, 1, **flag))
-    ck = op("g", [], lambda: g.iota(T.ck[:], [[K, 10]], 0, 0, **flag))
-    lt = op("g", [], lambda: g.iota(T.lt[:], [[1, C], [C, 16]], 0, 0, **flag))
     ones = op("v", [], lambda: v.memset(T.ones[:], 1.0))
     pj = op("v", [pi], ts(T.pj[:], T.pi[:], 15, None, A.bitwise_and))
-    co = op("v", [ones], lambda: v.tensor_tensor_scan(T.cnt[:], T.ones[:], T.ones[:], -1.0, A.add, A.mult))
-    mc = op("v", [pj], ts(T.mc[:], T.pj[:], float(CT + 3), None, A.is_lt))
-    p12 = op("v", [], ts(T.p12[:], T.pj[:], float(C), None, A.mult))
-    cut = op("v", [], ts(T.cut[:], T.pj[:], -float(K), None, A.mult))
-    gt = op("v", [co, pf], ts(T.gt[:], T.cnt[:, 0:128], T.pf[:], None, A.is_gt))
-    cl = op("v", [p12, ci], ts(T.cl[:, 0:C + 1], T.ci[:], T.p12[:], float(NT - 1), A.add, A.min))
-    op("v", [], ts(T.e0[:], T.cnt[:, 0:132], T.pf[:], float(LT), A.subtract, A.is_equal))
-    e1 = op("v", [], ts(T.e1[:], T.cnt[:, 0:132], T.pf[:], float(LT - 1), A.subtract, A.is_equal))
-    ma = op("v", [], ts(T.ma[:], T.pj[:], float(IA), None, A.is_equal))
+    co = op("v", [ones], lambda: v.tensor_tensor_scan(T.cnt[:], T.ones[:], T.ones[:], -K - 1.0, A.add, A.mult))
+    e0 = op("v", [xd], ts(T.e0[:], T.xd[:], float(LT), None, A.is_equal))
+    cut = op("v", [pj], ts(T.cut[:], T.pj[:], -float(K), None, A.mult))
+    pg = op("v", [], ts(T.pg[:], T.pi[:], 4, None, A.arith_shift_right))
     mb = op("v", [], ts(T.mb[:], T.pj[:], float(IB), None, A.is_equal))
-    qp = op("v", [e1], lambda: v.tensor_tensor(T.qp[:], T.e0[:], T.e1[:], A.subtract))
+    ma = op("v", [], ts(T.ma[:], T.pj[:], float(IA), None, A.is_equal))
     cb = op("v", [mb, ck], ts(T.cb[:], T.ck[:], T.mb[:], None, A.mult))
-    qn = op("v", [qp], ts(T.qn[:], T.qp[:], -1.0, None, A.mult))
-    mt = op("v", [], ts(T.mt[:], T.pj[:], float(TT), None, A.is_equal))
-    tri = op("g", [gt], lambda: g.affine_select(T.tri[:], T.gt[:], [[-16, 8], [0, 16]], A.is_ge, 0.0, 0, 1))
-    f0 = op("g", [ones], lambda: g.affine_select(T.f0[:], T.ones[:, 0:144], [[-16, 9], [-4096, 16]], A.is_ge, 0.0, 16, 1))
-    f1 = op("g", [f0], lambda: g.affine_select(T.f1[:], T.f0[:], [[16, 9], [-4096, 16]], A.is_ge, 0.0, 14 - 16, -1))
-    f = op("g", [f1], lambda: g.affine_select(T.f[:], T.f1[:], [[-16, 9], [0, 16]], A.not_equal, 0.0, 16 - (CT + 3), 1))
-    idi = op("g", [], lambda: g.iota(T.idi[:], [[16, LW]], NT, 0)) if mixed else None
+    p12 = op("s", [cut], lambda: s.activation(T.p12[:], T.cut[:], CP, scale=-C / K))
+    mc = op("s", [], lambda: s.activation(T.mc[:], T.cut[:], F.Relu, float((CT + 3) * K), 1.0))
+    cl = op("v", [p12, ci], ts(T.cl[:, 0:C + 1], T.ci[:], T.p12[:], float(NT - 1), A.add, A.min))
+    gt = op("v", [], ts(T.gt[:], T.xd[:, 0:128], 0.0, None, A.is_gt))
+    off = op("v", [pg], ts(T.off[:], T.pg[:], -float(P), -1.0, A.mult, A.add))
+    qp = op("g", [e0], lambda: g.affine_select(T.qp[:], T.e0[:], [[1, 132]], A.not_equal, -1.0, 1 - LT, -1))
+    lt = op("g", [], lambda: g.iota(T.lt[:], [[1, C], [C, 16]], 0, 0, **flag))
+    fc = T.f[:, 0:144:16]
+    f = op("g", [], lambda: g.affine_select(T.f[:], T.ones[:, 0:144], [[-16, 9], [-4096, 16]], A.is_ge, 0.0, 16, 1))
+    f = op("g", [f], lambda: g.affine_select(fc, fc, [[16, 9]], A.is_ge, 0.0, 14 - 16, -1))
+    f = op("g", [f], lambda: g.affine_select(fc, fc, [[-16, 9]], A.not_equal, 0.0, 16 - (CT + 3), 1))
 
-    def columns(q, deps, out, o, a, b):
-        while a < b:
-            k, e = a // K, min(b, (a // K + 1) * K)
-            src = T.cnt[:, a - K * k:e - K * k]
-            if q == "v":
-                t = op(q, deps, ts(out[:, o:o + e - a], src, T.ma[:], T.cb[:, k:k + 1], A.mult, A.add))
-            else:
-                t = op(q, deps, lambda: s.activation(out[:, o:o + e - a], src, ID, T.cb[:, k:k + 1], T.ma[:]))
-            o, a = o + e - a, e
-        return t
+    def columns(q, deps, out, k, a=0):
+        src = T.cnt[:, a:a + out.shape[1]]
+        if q == "v":
+            return op(q, deps, ts(out, src, T.ma[:], T.cb[:, k:k + 1], A.mult, A.add))
+        return op(q, deps, lambda: s.activation(out, src, ID, T.cb[:, k:k + 1], T.ma[:]))
 
-    dc = [op("s", [mc, ones], lambda: s.activation(T.d0[:, x:x + K], T.ones[:], CP, scale=T.mc[:])) for x in (0, K)][-1]
-    x1 = columns("s", [co, ma, cb], T.d1, 1280 - H, 1280, 2048)
-    sc = op("v", [("dl", 16), ones], lambda: v.tensor_tensor_scan(T.sc[:], T.lnb[:], T.ones[:, 0:C], 0.0, A.add, A.add))
+    columns("s", [co, ma, cb], T.d1[:, 0:B], 2)
+    x1 = columns("s", [], T.d1[:, B:2 * B], 3)
+    dc = [op("s", [mc], lambda: s.activation(T.d0[:, a:b], T.ones[:, 0:b - a], F.Sign, scale=T.mc[:])) for a, b in ((0, B), (B, W))][-1]
+    ia, ib = [[columns("s", [], w[:, H - B:H], 1), columns("s", [], w[:, 0:H - B], 0, 2 * B - H)][1] for w in (T.wa, T.wb)]
+    sc = op("v", [("dl", 16)], lambda: v.tensor_tensor_scan(T.sc[:], T.lnb[:], T.ones[:, 0:C], 0.0, A.add, A.add))
     rd = op("v", [cl, cut, ("dd", 48)], ts(T.rd[:], T.dsr[:, 0:NT].indirect(T.cl[:, 0:C + 1]), T.cut[:], 0.0, A.add, A.max))
-    sch = op("v", [sc], lambda: v.tensor_copy(T.sch[:], T.sc[:, C - 1:C]))
-    car = op("p", [tri, sch], lambda: pe.matmul(T.car[:, 0:1], T.tri[:], T.sch[:], True, True))
-    ct = op("v", [lt, mt], ts(T.ct[:], T.lt[:], T.mt[:], None, A.mult))
-    columns("v", [cb], T.d1, 0, H, 1280)
-    lasts = op("v", [car, sc], ts(T.lasts[:], T.sc[:], T.car[:, 0:1], -1.0, A.add, A.add))
-    x0 = columns("v", [], T.d1, 2048 - H, 2048, H + P)
-    op("p", [qn, rd], lambda: pe.matmul(T.zp[:, 0:NT], T.qn[:, LT:LT + 128], T.rd[:, 16:NT + 16], True, False))
-    op("p", [], lambda: pe.matmul(T.zp[:, 0:NT], T.qp[:, LT:LT + 128], T.rd[:, 0:NT], False, False))
-    zp = op("p", [], lambda: pe.matmul(T.zp[:, 0:NT], T.qp[:, 0:128], T.rd[:, 16:NT + 16], False, True))
-    ini = op("p", [], lambda: pe.matmul(T.ini[:, 0:1], T.qn[:, LT:LT + 128], T.rd[:, 0:1], True, True))
+    car = op("p", [gt, sc], lambda: pe.matmul(T.car[:, 0:1], T.gt[:], T.sc[:, C - 1:C], True, True))
+    qn = op("v", [qp], ts(T.qn[:], T.qp[:, LT:LT + 128], -1.0, None, A.mult))
+    lasts = op("v", [car, sc, off], ts(T.lasts[:], T.sc[:], T.car[:, 0:1], T.off[:], A.add, A.add))
+    ct = op("v", [lt, ma], ts(T.ct[:], T.lt[:], T.ma[:], None, A.mult))
+    x0 = columns("v", [cb], T.d1[:, 2 * B:P], 4)
+    op("p", [qp, rd], lambda: pe.matmul(T.zp[:, 0:NT], T.qp[:, LT:LT + 128], T.rd[:, 0:NT], True, False))
+    op("p", [], lambda: pe.matmul(T.zp[:, 0:NT], T.qp[:, 0:128], T.rd[:, 16:NT + 16], False, False))
+    zp = op("p", [qn], lambda: pe.matmul(T.zp[:, 0:NT], T.qn[:], T.rd[:, 16:NT + 16], False, True))
+    ini = op("p", [], lambda: pe.matmul(T.ini[:, 0:1], T.qn[:], T.rd[:, 0:1], True, True))
     z = op("v", [zp, ct], lambda: v.tensor_tensor(T.z[:], T.zp[:, 0:NT], T.ct[:], A.add))
     zs = op("v", [z, lasts, x0, x1], lambda: v.tensor_copy(T.d1[:, 0:P].indirect(T.lasts[:, 0:C]), T.z[:]))
     r = []
-    for a in range(0, P, B):
+    for a in (0, W):
         r.append(op("v", r[-1:] if r else [zs, dc, ini], lambda: v.tensor_tensor_scan(
-            T.wa[:, H + a:H + a + B], T.d0[:], T.d1[:, a:a + B], T.wa[:, H + a - 1:H + a] if a else T.ini[:, 0:1], A.mult, A.add)))
-    ia = [columns("v", [], T.wa, 0, 0, 2 * K), columns("s", [], T.wa, 2 * K, 2 * K, H)]
-    ib = columns("s", [], T.wb, 0, 0, H)
+            T.wa[:, H + a:H + a + W], T.d0[:], T.d1[:, a:a + W], T.wa[:, H + a - 1:H + a] if a else T.ini[:, 0:1], A.mult, A.add)))
 
     def ids(rs):
         out = []
@@ -174,118 +194,165 @@ def rank_program(g, core, T, topo):
             return [], e
         return e[:len(e) // 2], e[len(e) // 2:]
 
-    trs = []
-    for side, rs in ((0, [r for r in others if r > rank]), (1, [r for r in others if r < rank])):
-        if rs:
-            trs.append(RemoteDMATransfer(dst_ids=ids(rs), dma_engine_mask=bits(letter_engines(rank)[side]), remote_sem=S["la%d" % rank],
-                                         srcs=[T.dle[side]], dsts=[T.lel[rank] for _ in rs]))
+    takers = [sorted(rs, key=lambda r: -gathers_left(rank, r)) for rs in (range(N - 1, rank, -1), range(rank))]
+    trs = [RemoteDMATransfer(dst_ids=ids(rs), dma_engine_mask=bits(letter_engines(rank)[side]), remote_sem=S["la%d" % rank],
+                             srcs=[T.dle[side]], dsts=[T.lel[rank] for _ in rs]) for side, rs in enumerate(takers) if rs]
     g.wait_ge(S.dle, 16)
     g.remote_dma_fused(trs, local_sem=S.ls)
     sent = sum(len(e) for e in letter_engines(rank))
 
-    blank = [(k, side) for k in range(n) for side in range(2) if stage[k][side] is None]
-    zero = blank if mixed else blank[1:]
-    need("y", op("v", [], lambda: v.memset(T.yo[:, 0:W], 0.0)))
-    sync.dma_start(sw[0][:, NT:H], T.yo[:, 0:W]).then_inc(S.lz, 16)
-    for k, side in zero:
-        sync.dma_start(sw[k][half(side), 0:NT], T.yo[half(side), 0:NT]).then_inc(S.lz, 16)
-    z0 = ("lz", 16 + 16 * len(zero) + (16 * len(blank) if mixed else 0))
-    if mixed:
-        pm = op("v", [], lambda: v.tensor_copy(T.pm[:], T.pj[:]))
-        need("y", op("v", [idi, pm], ts(T.idl[:], T.idi[:], T.pm[:], None, A.add)))
-        for k, side in blank:
-            sync.dma_start(T.cl5[half(side), LW * k:LW * k + LW], T.idl[half(side), :]).then_inc(S.lz, 16)
+    for dst, side in own:
+        sync.dma_start(dst, T.le[half(side), :]).then_inc(S.lo, 16)
+    need("y", f)
+    for x, o, a, b in ((0, 0, 0, 80), (0, 80, 16, 80), (1, 0, 64, 144), (1, 80, 80, 144)):
+        sync.dma_start(T.f2[half(x), o:o + b - a], T.f[half(x), a:b]).then_inc(S.df, 16)
+    zeros = [T.sw[:, NT:H]]
+    if end:
+        zeros.append(T.se[:, NT:H])
+    else:
+        used = [slot(sh, k) for k in range(m + 1)]
+        zeros += [letters(sh, k) for k in range(n + 1) if k not in used]
+    for x in zeros:
+        z0 = op("g", [("cg", cnt["g"])], lambda: g.iota(x, [[0, x.shape[1]]], 0, 0, **flag))
+    landed = 0
+    for (side, k), src in sorted(source.items(), key=lambda x: call_of(x[1], rank)):
+        need("y", ("la%d" % src, len(letter_engines(src)[side])))
+        for x in (range(2) if end else [side]):
+            sync.dma_start(letters(x, slot(side, k)), T.lel[src]).then_inc(S.lw, 16)
+            landed += 16
 
-    def conv(deps, out, win, a, b):
+    def conv(deps, out, win, a, b, side=None):
         need("p", *deps)
+        fm, rows = (T.f, slice(0, 128)) if side is None else (T.f2, half(side))
         for q in range(16):
-            t = op("p", [], lambda: pe.matmul(out[:, a // 16:b // 16], T.f[:, 16 - q:144 - q], win[:, H + a + q:H + b:16], q == 0, q == 15))
+            t = op("p", [], lambda: pe.matmul(out[:, a // 16:b // 16], fm[rows, 16 - q:144 - q], win[rows, H + a + q:H + b:16], q == 0, q == 15))
         return t
 
-    def emit(dep, out, a, b, src):
-        return op("v", [dep], lambda: v.tensor_copy(out[:, a:b], src[:, a:b]))
+    def emit(deps, out, src, add=None):
+        if add is None:
+            return op("v", deps, lambda: v.tensor_copy(out, src))
+        return op("v", deps, ts(out, src, add, None, A.add))
 
-    def jump(deps, out, o, win, lst, a, b):
-        h = (a + b) // 2
+    def jump(deps, out, o, win, z, lst, a, b, vc=None):
+        h = a + ((b - a) // 2 if vc is None else vc)
         e = o + 16 * (h - a)
-        z = win.shape[1]
         t1 = op("v", deps, lambda: v.tensor_copy(out[:, o:e], win[:, 0:z].indirect(lst[:, a:h])))
         t2 = op("s", deps, lambda: s.activation(out[:, e:o + 16 * (b - a)], win[:, 0:z].indirect(lst[:, h:b]), CP))
         return [t1, t2]
 
-    full, BC = P // 16, B // 16
-    win, oth, lst, nxt = T.wa, T.wb, T.la, T.lb
-    c1, c2 = conv([r[0], f], T.cva, win, 0, B), conv(r[-1:], T.cvb, win, B, P)
-    ready = r[-1:] + ia
-    cols = ((0, BC), (BC, full))
-    later = ((LW, full), (0, LW))
-    for i, (a, b) in enumerate((cols, later, later, later)):
-        e1 = emit(c1, lst, cols[0][0], cols[0][1], T.cva)
-        t1 = jump(ready + [e1], oth, H + 16 * a[0], win, lst, a[0], a[1]) if i != 1 else None
-        e2 = emit(c2, lst, cols[1][0], cols[1][1], T.cvb)
-        if t1 is None:
-            t1 = jump(ready + [e1, e2], oth, H + 16 * a[0], win, lst, a[0], a[1])
-        c1 = conv(t1, T.cva, oth, 16 * a[0], 16 * a[1])
-        t2 = jump([e2], oth, H + 16 * b[0], win, lst, b[0], b[1])
-        c2 = conv(t2, T.cvb, oth, 16 * b[0], 16 * b[1])
-        ready = t1 + t2
-        win, oth = oth, win
-        if i == 0:
-            ready = jump(ready + [ib], oth, H, win, lst, 0, full)
-            win, oth = oth, win
-        lst, nxt = nxt, lst
-        cols = (a, b)
-    e1 = emit(c1, lst, cols[0][0], cols[0][1], T.cva)
-    t = jump(ready + [e1], oth, H + W, win, lst, LW, full)
-    cp = conv(t, T.cva, oth, W, P)
-    e2 = emit(c2, lst, cols[1][0], cols[1][1], T.cvb)
-    t = jump([e2], oth, H, win, lst, 0, LW)
-    cq = conv(t, T.cvb, oth, 0, W)
-    tail = emit(cp, T.ol, LW, full, T.cva)
-    te = []
-    if not mixed:
-        te += jump([tail, z0, ("lo", 32), ("lw", 16 * (up + down))], T.ye, W, sw[0], T.ol, LW, full)
-    head = emit(cq, T.ol, 0, LW, T.cvb)
-    if not mixed:
-        te += jump([head], T.ye, 0, sw[0], T.ol, 0, LW)
+    full = P // 16
+    head, tail = slice(0, LW), slice(LW, full)
+    wins, bank = (T.wa, T.wb), (T.cvb, T.cva)
+    wrote = {(0, 0): [r[0], ia], (0, 1): [r[1]], (1, 0): [ib], (1, 1): []}
+    read = {x: [] for x in wrote}
+    latest, turned, listed = [0, 0], [None, None], [None, None]
 
-    need("g", tail)
-    g.remote_dma_fused([RemoteDMATransfer(dst_ids=ids(others), dma_engine_mask=bits(shared(rank)), remote_sem=S["ar%d" % rank],
-                                          srcs=[T.ol[:, LW:full]], dsts=[T.ll[:, LW * rank:LW * rank + LW] for _ in others])], local_sem=S.ls)
-    sent += len(shared(rank))
+    def turn(x):
+        turned[x] = conv(wrote[latest[x], x] + [f], bank[x], wins[latest[x]], W * x, W * x + W)
+        read[latest[x], x].append(turned[x])
 
-    for k in range(n):
-        for side in range(2):
-            src = stage[k][side]
-            if src is not None:
-                need("y", ("la%d" % src, len(letter_engines(src)[side])))
-                sync.dma_start(sw[k][half(side), 0:NT], T.lel[src]).then_inc(S.lw, 16)
-    stored = 0
-    if not mixed:
-        need("y", *te)
-        sync.dma_start(T.y[half(own), :], T.ye[half(own), :]).then_inc(S.st, 16)
-        stored += 16
+    def gather(x, vc):
+        if turned[x]:
+            listed[x], turned[x] = emit([turned[x]], T.la[:, LW * x:LW * x + LW], bank[x][:, LW * x:LW * x + LW]), None
+        w = latest[x]
+        deps = [d for y in range(x + 1) for d in wrote[w, y]] + read[1 - w, x] + [listed[x]]
+        t = jump(deps, wins[1 - w], H + W * x, wins[w], H + W * x + W, T.la, LW * x, LW * x + LW, vc)
+        for y in range(x + 1):
+            read[w, y] += t
+        wrote[1 - w, x], read[1 - w, x], latest[x] = t + wrote[1 - w, x][-1:], [], 1 - w
+        return t
 
-    ready = [z0, ("lw", 16 * (up + down))]
-    for k in range(n):
-        if mixed:
-            for side in range(2):
-                src = stage[k][side]
-                if src is not None:
-                    ready.append(op("v", [("ar%d" % src, len(shared(src)))], lambda: v.tensor_copy(
-                        T.cl5[half(side), LW * k:LW * k + LW], T.ll[half(side), LW * src:LW * src + LW])))
-            lst, a = T.cl5, LW * k
+    turn(0)
+    turn(1)
+    for i, (x, turns) in enumerate(PLAN):
+        y = PLAN[i + 1][0] if i + 1 < len(PLAN) else 1
+        gather(x, VC if y != x and turned[y] else None)
+        if turns:
+            turn(x)
+
+    t = gather(1, None)
+    ps = {sh: T.cva, lg: T.cvc}
+    so = [T.so[:, LW * x:LW * x + LW] for x in range(2)]
+    ctail = {sh: conv(t + [("df", 64)], ps[sh], wins[latest[1]], W, P, sh)}
+    if not end:
+        ctail[lg] = conv([], ps[lg], wins[latest[1]], W, P, lg)
+
+    def send(side):
+        need("g", emit([ctail[side]], so[side], ps[side][:, tail], float(H * piece(rank, side))))
+        g.remote_dma_fused([RemoteDMATransfer(dst_ids=ids(takers[side]), dma_engine_mask=bits(shared(rank)), remote_sem=S["ar%d" % rank],
+                                              srcs=[so[side]], dsts=[T.ll[:, LW * rank:LW * rank + LW] for _ in takers[side]])], local_sem=S.ls)
+        return len(shared(rank))
+
+    t = gather(0, VC - 4)
+    sent += send(sh)
+    chead = conv(t, T.cvb, wins[latest[0]], 0, W)
+    if end:
+        ctail[lg] = conv([], ps[lg], wins[latest[1]], W, P, lg)
+    else:
+        sent += send(lg)
+
+    stored = [0]
+
+    def store(q, deps, rows, a, src):
+        need(q, *deps)
+        queue[q].dma_start(T.y[rows, a:a + src.shape[1]], src).then_inc(S.st, 16)
+        stored[0] += 16
+
+    if end:
+        emit([], T.ol[half(lg), head], ps[sh][half(lg), tail])
+        e = emit([chead], T.ol[half(sh), head], T.cvb[half(sh), head])
+        t = jump([e, z0, ("lo", 16 * len(own))], T.yo, W, T.se, H, T.ol, 0, LW, VC - 2)
+        store("y", t + [("ls", sent)], half(sh), 0, T.yo[half(sh), W:P])
+        store("y", t, half(sh), W, T.yo[half(lg), W:P])
+        emit([], T.ol[half(lg), tail], T.cvb[half(lg), head], float(H * n))
+        mine = emit([ctail[lg]], T.ol[half(sh), tail], ps[lg][half(sh), tail], float(H * n))
+    else:
+        if spare == 1:
+            emit([chead], T.ol[half(lg), head], T.cvb[half(lg), head], float(H * n))
+            mine = emit([], T.ol[half(sh), head], ps[sh][half(sh), tail], float(H * slot(sh, m)))
         else:
-            src = stage[k][1 - own]
-            ready.append(("ar%d" % src, len(shared(src))))
-            lst, a = T.ll, LW * src
-        ready = jump(ready, sw[k + 1], NT, sw[k], lst, a, a + LW)
-    ready += [head, ("lo", 16 if mixed else 32)]
-    rows = slice(0, 128) if mixed else half(1 - own)
-    for a, b in ((0, 32), (32, 64), (64, 96)):
-        t = jump(ready, T.yo, 16 * a, sw[n], T.ol, a, b)
-        need("y", *t)
-        sync.dma_start(T.y[rows, 16 * a:16 * b], T.yo[rows, 16 * a:16 * b]).then_inc(S.st, 16)
-        stored += 16
+            mine = emit([chead], T.ol[:, head], T.cvb[:, head], float(H * n))
+        if spare == 0:
+            emit([], T.ol[half(lg), tail], ps[lg][half(lg), tail], float(H * n))
+            mine = emit([], T.ol[half(sh), tail], ps[sh][half(sh), tail], float(H * n))
+
+    def arrived(src):
+        return ("ar%d" % src, len(shared(src)))
+
+    def short(k):
+        if end or not lagged <= k < n:
+            return []
+        dst = T.ll[half(sh), LW * source[lg, k]:LW * source[lg, k] + LW]
+        deps, j = [arrived(source[lg, k])], k - lagged
+        if j < m:
+            src = source[sh, j]
+            return [emit(deps + [arrived(src)], dst, T.ll[half(sh), LW * src:LW * src + LW], float(H * (slot(sh, j) - j)))]
+        return [emit(deps, dst, T.cvb[half(sh), head] if j == m else ps[sh][half(sh), tail], float(H * slot(sh, m)))]
+
+    ready = [z0, ("lw", landed), ("lo", 16 * len(own))] + short(0)
+    for k in range(n):
+        src = source[lg, k]
+        more = not end and lagged <= k + 1 < n
+        ready = jump(ready + [arrived(src)], T.sw, H * (k + 1) + NT, T.sw, H * (k + 1), T.ll, LW * src, LW * src + LW, VC if more else None)
+        if not end and k >= lagged + m:
+            store("y", ready, half(sh), W * (k - lagged - m), T.sw[half(sh), H * (k + 1) + NT:H * (k + 2)])
+        ready = ready + short(k + 1)
+
+    ready.append(mine)
+    if end:
+        t = jump(ready, T.yo, 0, T.sw, H * (n + 1), T.ol, LW, full)
+        store("y", t, half(lg), 0, T.yo[half(lg), 0:W])
+        store("s", t, half(lg), W, T.yo[half(sh), 0:W])
+    elif spare:
+        t = jump(ready, T.yo, 0, T.sw, H * (n + 1), T.ol, 0, LW)
+        store("y", t, half(lg), 0, T.yo[half(lg), 0:W])
+        if spare == 1:
+            store("y", t, half(sh), W, T.yo[half(sh), 0:W])
+        t = jump(ready, T.yo, W, T.sw, H * (n + 1), T.so, LW * lg, LW * lg + LW)
+        store("y", t, half(lg), W, T.yo[half(lg), W:P])
+    else:
+        for a, b in ((0, 16), (16, LW), (LW, full)):
+            t = jump(ready, T.yo, 16 * a, T.sw, H * (n + 1), T.ol, a, b)
+            store("y", t, slice(0, 128), 16 * a, T.yo[:, 16 * a:16 * b])
     g.wait_ge(S.ls, sent)
-    need("y", ("st", stored), *[("c" + q, cnt[q]) for q in cnt])
+    need("y", ("st", stored[0]), *[("c" + q, cnt[q]) for q in cnt])

@@ -7,25 +7,29 @@ C = NT // 16
 LW = W // 16
 B = P // 3
 K = 256
-CT, LT, IA, IB = 0, 4, 8, 9
+HT = NT // 2
+FW = 144
+RAW, CANCEL = 1, 3
+FOURS = 1.5 * 2 ** 25
 VC = 22
-PLAN = [(0, 1), (1, 0), (1, 1), (0, 0), (0, 1), (1, 0), (1, 1), (0, 1), (1, 1), (0, 0)]
-LAG, LAST = {5: 0, 4: 2, 3: 1}, {5: 0.6, 4: 0.4, 3: 1.0}
+PLAN = [(0, 1, 22, 14), (1, 0, 24, None), (1, 1, 22, 6), (0, 0, 24, None), (0, 1, 22, 6), (1, 0, 24, None), (1, 1, 22, 6),
+        (0, 0, 24, 24), (1, 1, 24, None), (0, 1, 24, 24), (1, 0, 24, 24)]
+SHARE = {"last": 16}
+LAG, LAST = {5: 0, 4: 3, 3: 1}, {5: 0.6, 4: 0.4, 3: 1.0}
 SCRATCH = {
-    "lnb": ("sbuf", [128, C], "int32"), "dsr": ("sbuf", [128, NT], "int32"),
+    "lnb": ("sbuf", [128, C], "int32"), "dsr": ("sbuf", [128, HT + 8], "int32"),
     "sc": ("sbuf", [128, C], "float16"),
-    "lasts": ("sbuf", [128, C], "uint16"), "ci": ("sbuf", [128, C + 1], "int32"), "cl": ("sbuf", [128, C + 2], "uint16"),
-    "pi": ("sbuf", [128, 1], "int32"), "pj": ("sbuf", [128, 1], "int32"), "xd": ("sbuf", [128, 132], "bfloat16"),
-    "cut": ("sbuf", [128, 1], "float32"), "p12": ("sbuf", [128, 1], "float32"), "mc": ("sbuf", [128, 1], "float32"),
-    "ma": ("sbuf", [128, 1], "float32"), "mb": ("sbuf", [128, 1], "float32"),
-    "pg": ("sbuf", [128, 1], "int32"), "off": ("sbuf", [128, 1], "float32"),
-    "ck": ("sbuf", [128, 5], "float32"), "cb": ("sbuf", [128, 5], "float32"),
+    "lasts": ("sbuf", [128, C], "uint16"), "cl": ("sbuf", [128, 8], "uint16"),
+    "pi": ("sbuf", [128, 1], "int32"), "pj": ("sbuf", [128, 1], "int32"), "xd": ("sbuf", [128, 140], "bfloat16"),
+    "p2": ("sbuf", [128, 1], "int32"), "p6": ("sbuf", [128, 1], "float32"), "mc": ("sbuf", [128, 1], "float32"),
+    "ma": ("sbuf", [128, 1], "float32"), "mb": ("sbuf", [128, 1], "float32"), "mr": ("sbuf", [128, 1], "float32"),
+    "p96": ("sbuf", [128, 1], "float32"), "off": ("sbuf", [128, 1], "float32"), "cb": ("sbuf", [128, 5], "float32"),
     "ones": ("sbuf", [128, B], "bfloat16"), "cnt": ("sbuf", [128, B], "bfloat16"),
-    "e0": ("sbuf", [128, 132], "float16"), "qp": ("sbuf", [128, 132], "float16"), "qn": ("sbuf", [128, 128], "float16"),
-    "gt": ("sbuf", [128, 128], "float16"),
-    "f": ("sbuf", [128, 144], "bfloat16"), "f2": ("sbuf", [128, 144], "bfloat16"),
-    "lt": ("sbuf", [128, NT], "bfloat16"), "ct": ("sbuf", [128, NT], "bfloat16"),
-    "rd": ("sbuf", [128, NT + 16], "float16"), "z": ("sbuf", [128, NT], "bfloat16"),
+    "e0": ("sbuf", [128, 140], "bfloat16"), "qp": ("sbuf", [128, 140], "bfloat16"), "qn": ("sbuf", [128, 136], "bfloat16"),
+    "gt": ("sbuf", [128, 128], "float16"), "dg": ("sbuf", [128, 128], "bfloat16"),
+    "fc": ("sbuf", [128, 9], "bfloat16"), "f": ("sbuf", [128, 2 * FW], "bfloat16"), "f2": ("sbuf", [128, FW], "bfloat16"),
+    "lt": ("sbuf", [128, NT], "bfloat16"),
+    "rd": ("sbuf", [128, HT + 16], "float16"), "z": ("sbuf", [128, NT], "bfloat16"),
     "d0": ("sbuf", [128, W], "bfloat16"), "d1": ("sbuf", [128, P], "bfloat16"),
     "wa": ("sbuf", [128, H + P], "bfloat16"), "wb": ("sbuf", [128, H + P], "bfloat16"),
     "la": ("sbuf", [128, P // 16], "uint16"),
@@ -33,10 +37,11 @@ SCRATCH = {
     "sw": ("sbuf", [128, N * H], "bfloat16"), "se": ("sbuf", [128, H], "bfloat16"),
     "yo": ("sbuf", [128, P], "bfloat16"),
     "dle": ("dram", [2, 128, NT // 2], "bfloat16"), "lel": ("dram", [N, 128, NT // 2], "bfloat16"),
-    "car": ("psum", [128, 512], "float32"), "zp": ("psum", [128, 512], "float32"), "ini": ("psum", [128, 512], "float32"),
+    "car": ("psum", [128, 512], "float32"), "ini": ("psum", [128, 512], "float32"),
+    "zpa": ("psum", [128, 32, 16], "float32"), "zpb": ("psum", [128, 32, 16], "float32"),
     "cva": ("psum", [128, 512], "float32"), "cvb": ("psum", [128, 512], "float32"), "cvc": ("psum", [128, 512], "float32"),
 }
-SEMAPHORES = ["cg", "cv", "cs", "cp", "dl", "dd", "dle", "lo", "lw", "df", "st", "ls"]
+SEMAPHORES = ["cg", "cv", "cs", "cp", "dl", "dd", "dle", "lo", "lw", "st", "ls"]
 SEMAPHORES += ["ar%d" % k for k in range(N)] + ["la%d" % k for k in range(N)]
 
 
@@ -88,6 +93,9 @@ def rank_program(g, core, T, topo):
     def ts(out, in0, s1, s2, *ops):
         return lambda: v.tensor_scalar(out, in0, s1, s2, *ops)
 
+    def mm(deps, out, lhs, rhs, first, last):
+        return op("p", deps, lambda: pe.matmul(out, lhs, rhs, first, last))
+
     def half(side):
         return slice(64 * side, 64 * side + 64)
 
@@ -109,9 +117,8 @@ def rank_program(g, core, T, topo):
     dz = op("v", [], lambda: v.memset(T.dsr[:], 0))
     need("y", dz)
     need("s", dz)
-    sync.dma_start(T.dsr[CT:128:16, :], T.ds[:]).then_inc(S.dd, 16)
-    s.dma_start(T.dsr[CT + 1:128:16, :], T.ds[:]).then_inc(S.dd, 16)
-    sync.dma_start(T.dsr[CT + 2:128:16, :], T.ds[:]).then_inc(S.dd, 16)
+    s.dma_start(T.dsr[RAW:128:8, 0:HT], T.ds[:]).then_inc(S.dd, 16)
+    sync.dma_start(T.dsr[RAW + 1:128:8, 0:HT], T.ds[:]).then_inc(S.dd, 16)
     sync.dma_start(T.dle[:], T.le[:]).then_inc(S.dle, 16)
     if end:
         own = [(letters(x, n), lg) for x in range(2)] + [(T.se[half(x), 0:NT], sh) for x in range(2)]
@@ -120,29 +127,31 @@ def rank_program(g, core, T, topo):
 
     flag = {"allow_small_or_imprecise_dtypes": True}
     pi = op("g", [], lambda: g.iota(T.pi[:], [[1, 1]], 0, 1))
-    xd = op("g", [], lambda: g.iota(T.xd[:], [[1, 132]], 0, -1, **flag))
-    ck = op("g", [], lambda: g.iota(T.ck[:], [[B, 5]], H - 2 * B + K, 0, **flag))
-    ci = op("g", [], lambda: g.iota(T.ci[:], [[1, C + 1]], 0, 0))
+    xd = op("g", [], lambda: g.iota(T.xd[:], [[1, 140]], 0, -1, **flag))
+    lt = op("g", [], lambda: g.iota(T.lt[:], [[1, C], [C, 16]], 0, 0, **flag))
     ones = op("v", [], lambda: v.memset(T.ones[:], 1.0))
     pj = op("v", [pi], ts(T.pj[:], T.pi[:], 15, None, A.bitwise_and))
+    p2 = op("v", [], ts(T.p2[:], T.pi[:], RAW + 1, None, A.bitwise_and))
     co = op("v", [ones], lambda: v.tensor_tensor_scan(T.cnt[:], T.ones[:], T.ones[:], -K - 1.0, A.add, A.mult))
-    e0 = op("v", [xd], ts(T.e0[:], T.xd[:], float(LT), None, A.is_equal))
-    cut = op("v", [pj], ts(T.cut[:], T.pj[:], -float(K), None, A.mult))
-    pg = op("v", [], ts(T.pg[:], T.pi[:], 4, None, A.arith_shift_right))
-    mb = op("v", [], ts(T.mb[:], T.pj[:], float(IB), None, A.is_equal))
-    ma = op("v", [], ts(T.ma[:], T.pj[:], float(IA), None, A.is_equal))
-    cb = op("v", [mb, ck], ts(T.cb[:], T.ck[:], T.mb[:], None, A.mult))
-    p12 = op("s", [cut], lambda: s.activation(T.p12[:], T.cut[:], CP, scale=-C / K))
-    mc = op("s", [], lambda: s.activation(T.mc[:], T.cut[:], F.Relu, float((CT + 3) * K), 1.0))
-    cl = op("v", [p12, ci], ts(T.cl[:, 0:C + 1], T.ci[:], T.p12[:], float(NT - 1), A.add, A.min))
+    e0 = op("v", [xd], ts(T.e0[:], T.xd[:], float(CANCEL), None, A.is_equal))
+    mb = op("v", [pj], ts(T.mb[:], T.pj[:], float(RAW + CANCEL + 1), float(K), A.is_equal, A.mult))
+    p6 = op("v", [], ts(T.p6[:], T.pj[:], float(C // 2), None, A.mult))
+    ma = op("v", [], ts(T.ma[:], T.pj[:], float(RAW + CANCEL), None, A.is_equal))
+    mr = op("v", [p2], ts(T.mr[:], T.p2[:], FOURS / (RAW + 1), None, A.mult))
     gt = op("v", [], ts(T.gt[:], T.xd[:, 0:128], 0.0, None, A.is_gt))
-    off = op("v", [pg], ts(T.off[:], T.pg[:], -float(P), -1.0, A.mult, A.add))
-    qp = op("g", [e0], lambda: g.affine_select(T.qp[:], T.e0[:], [[1, 132]], A.not_equal, -1.0, 1 - LT, -1))
-    lt = op("g", [], lambda: g.iota(T.lt[:], [[1, C], [C, 16]], 0, 0, **flag))
-    fc = T.f[:, 0:144:16]
-    f = op("g", [], lambda: g.affine_select(T.f[:], T.ones[:, 0:144], [[-16, 9], [-4096, 16]], A.is_ge, 0.0, 16, 1))
-    f = op("g", [f], lambda: g.affine_select(fc, fc, [[16, 9]], A.is_ge, 0.0, 14 - 16, -1))
-    f = op("g", [f], lambda: g.affine_select(fc, fc, [[-16, 9]], A.not_equal, 0.0, 16 - (CT + 3), 1))
+    cb = op("v", [mb, co], ts(T.cb[:], T.cnt[:, K:K + 10:2], (H - 2 * B + K) / K, T.mb[:], A.add, A.mult))
+    cl = op("v", [p6], ts(T.cl[:, 0:7], T.cnt[:, K:K + 7], T.p6[:], None, A.add))
+    dg = op("v", [ma], ts(T.dg[:], T.xd[:, 0:128], 0.0, T.ma[:], A.is_equal, A.mult))
+    f0 = op("s", [ones], lambda: s.activation(T.f[:], T.ones[:, 0:2 * FW], CP, scale=0.0))
+    p96 = op("s", [xd], lambda: s.activation(T.p96[:], T.xd[:, 0:1], CP, -1.0, float(P // 16)))
+    mc = op("s", [p6], lambda: s.activation(T.mc[:], T.p6[:], F.Relu, (RAW + 1.5) * C / 2, -1.0))
+    off = op("s", [p96], lambda: s.activation(T.off[:], T.p6[:], ID, T.p96[:], 16.0))
+    qp = op("g", [e0], lambda: g.affine_select(T.qp[:], T.e0[:], [[1, 140]], A.not_equal, -1.0, 1 - CANCEL, -1))
+    f = op("g", [ones], lambda: g.affine_select(T.fc[:], T.ones[:, 0:9], [[-16, 9]], A.is_ge, 0.0, 16 - RAW, 1))
+    f = op("g", [f], lambda: g.affine_select(T.fc[:], T.fc[:], [[16, 9]], A.is_ge, 0.0, RAW + CANCEL + 1 - 16, -1))
+    op("g", [f, f0], lambda: g.affine_select(T.f[:, FW + 1:2 * FW:16], T.fc[:], [[16, 9]], A.is_ge, 0.0, RAW + 1 - 16, -1))
+    for a in (FW, 0):
+        f = op("g", [], lambda: g.affine_select(T.f[:, a:a + FW:16], T.fc[:], [[-16, 9]], A.not_equal, 0.0, 16 - (RAW + CANCEL - 1), 1))
 
     def columns(q, deps, out, k, a=0):
         src = T.cnt[:, a:a + out.shape[1]]
@@ -150,26 +159,44 @@ def rank_program(g, core, T, topo):
             return op(q, deps, ts(out, src, T.ma[:], T.cb[:, k:k + 1], A.mult, A.add))
         return op(q, deps, lambda: s.activation(out, src, ID, T.cb[:, k:k + 1], T.ma[:]))
 
+    def carry(q, deps, a, b):
+        if q == "v":
+            return op(q, deps, ts(T.d0[:, a:b], T.ones[:, 0:b - a], T.mc[:], 0.0, A.mult, A.is_gt))
+        return op(q, deps, lambda: s.activation(T.d0[:, a:b], T.ones[:, 0:b - a], F.Sign, scale=T.mc[:]))
+
+    zp = (T.zpa, T.zpb)
     columns("s", [co, ma, cb], T.d1[:, 0:B], 2)
     x1 = columns("s", [], T.d1[:, B:2 * B], 3)
-    dc = [op("s", [mc], lambda: s.activation(T.d0[:, a:b], T.ones[:, 0:b - a], F.Sign, scale=T.mc[:])) for a, b in ((0, B), (B, W))][-1]
-    ia, ib = [[columns("s", [], w[:, H - B:H], 1), columns("s", [], w[:, 0:H - B], 0, 2 * B - H)][1] for w in (T.wa, T.wb)]
+    for u in range(2):
+        mm([dg, lt], zp[u][:, 0:C // 2, :], T.dg[:], T.lt[:, HT * u:HT * u + HT], True, False)
     sc = op("v", [("dl", 16)], lambda: v.tensor_tensor_scan(T.sc[:], T.lnb[:], T.ones[:, 0:C], 0.0, A.add, A.add))
-    rd = op("v", [cl, cut, ("dd", 48)], ts(T.rd[:], T.dsr[:, 0:NT].indirect(T.cl[:, 0:C + 1]), T.cut[:], 0.0, A.add, A.max))
-    car = op("p", [gt, sc], lambda: pe.matmul(T.car[:, 0:1], T.gt[:], T.sc[:, C - 1:C], True, True))
-    qn = op("v", [qp], ts(T.qn[:], T.qp[:, LT:LT + 128], -1.0, None, A.mult))
-    lasts = op("v", [car, sc, off], ts(T.lasts[:], T.sc[:], T.car[:, 0:1], T.off[:], A.add, A.add))
-    ct = op("v", [lt, ma], ts(T.ct[:], T.lt[:], T.ma[:], None, A.mult))
+    car = mm([gt, sc], T.car[:, 0:1], T.gt[:], T.sc[:, C - 1:C], True, True)
+    rd = op("v", [cl, mr, ("dd", 32)], ts(T.rd[:], T.dsr[:].indirect(T.cl[:, 0:7]), T.mr[:], T.mr[:], A.add, A.subtract))
+    qn = op("v", [qp], lambda: v.tensor_tensor(T.qn[:], T.qp[:, 0:136], T.qp[:, CANCEL:CANCEL + 136], A.subtract))
     x0 = columns("v", [cb], T.d1[:, 2 * B:P], 4)
-    op("p", [qp, rd], lambda: pe.matmul(T.zp[:, 0:NT], T.qp[:, LT:LT + 128], T.rd[:, 0:NT], True, False))
-    op("p", [], lambda: pe.matmul(T.zp[:, 0:NT], T.qp[:, 0:128], T.rd[:, 16:NT + 16], False, False))
-    zp = op("p", [qn], lambda: pe.matmul(T.zp[:, 0:NT], T.qn[:], T.rd[:, 16:NT + 16], False, True))
-    ini = op("p", [], lambda: pe.matmul(T.ini[:, 0:1], T.qn[:], T.rd[:, 0:1], True, True))
-    z = op("v", [zp, ct], lambda: v.tensor_tensor(T.z[:], T.zp[:, 0:NT], T.ct[:], A.add))
-    zs = op("v", [z, lasts, x0, x1], lambda: v.tensor_copy(T.d1[:, 0:P].indirect(T.lasts[:, 0:C]), T.z[:]))
+    lasts = op("v", [car, sc, off], ts(T.lasts[:], T.sc[:], T.car[:, 0:1], T.off[:], A.add, A.add))
+    hc, zz = C // 2, []
+    for x in range(2):
+        for u in range(2):
+            mm([qp, rd], zp[x][:, 0:hc, 8 * u:8 * u + 8], T.qp[:, CANCEL + 8 * u:CANCEL + 8 * u + 128], T.rd[:, x:HT:2], False, False)
+    mm([qn], T.zpb[:, hc - 1, 7:8], T.qn[:, 8:136], T.rd[:, 0:1], False, False)
+    for x in (1, 0):
+        for u in range(2):
+            t = mm([], zp[x][:, 0:hc, 8 * u:8 * u + 8], T.qn[:, 8 * u:8 * u + 128], T.rd[:, 16 + x:HT + 16:2], False, u == 1)
+        zz.append(t)
+    ini = mm([], T.ini[:, 0:1], T.qn[:, 0:128], T.rd[:, 0:1], True, True)
+    zb = op("s", zz[:1], lambda: s.activation(T.z[:, HT:NT], T.zpb[:, 0:hc, :], CP))
+    za = op("v", zz[1:], lambda: v.tensor_copy(T.z[:, 0:HT], T.zpa[:, 0:hc, :]))
+    dv = carry("v", [mc], B, W)
+    dc = carry("s", [ones, mc], 0, B)
+    columns("s", [], T.wa[:, H - B:H], 1)
+    ia = columns("s", [], T.wa[:, 0:H - B], 0, 2 * B - H)
+    ib = [columns("s", [], T.wb[:, 0:H - B - K], 0, 2 * B - H)]
+    zs = op("v", [za, zb, lasts, x0, x1], lambda: v.tensor_copy(T.d1[:, 0:P].indirect(T.lasts[:, 0:C]), T.z[:]))
     r = []
-    for a in (0, W):
-        r.append(op("v", r[-1:] if r else [zs, dc, ini], lambda: v.tensor_tensor_scan(
+    for a, o in ((0, 0), (W, K)):
+        columns("v", [], T.wb[:, H - B + o:H - B + o + K], 1, o)
+        r.append(op("v", r[-1:] if r else [zs, dc, dv, ini], lambda: v.tensor_tensor_scan(
             T.wa[:, H + a:H + a + W], T.d0[:], T.d1[:, a:a + W], T.wa[:, H + a - 1:H + a] if a else T.ini[:, 0:1], A.mult, A.add)))
 
     def ids(rs):
@@ -194,6 +221,8 @@ def rank_program(g, core, T, topo):
             return [], e
         return e[:len(e) // 2], e[len(e) // 2:]
 
+    for dst, side in own:
+        sync.dma_start(dst, T.le[half(side), :]).then_inc(S.lo, 16)
     takers = [sorted(rs, key=lambda r: -gathers_left(rank, r)) for rs in (range(N - 1, rank, -1), range(rank))]
     trs = [RemoteDMATransfer(dst_ids=ids(rs), dma_engine_mask=bits(letter_engines(rank)[side]), remote_sem=S["la%d" % rank],
                              srcs=[T.dle[side]], dsts=[T.lel[rank] for _ in rs]) for side, rs in enumerate(takers) if rs]
@@ -201,11 +230,8 @@ def rank_program(g, core, T, topo):
     g.remote_dma_fused(trs, local_sem=S.ls)
     sent = sum(len(e) for e in letter_engines(rank))
 
-    for dst, side in own:
-        sync.dma_start(dst, T.le[half(side), :]).then_inc(S.lo, 16)
-    need("y", f)
     for x, o, a, b in ((0, 0, 0, 80), (0, 80, 16, 80), (1, 0, 64, 144), (1, 80, 80, 144)):
-        sync.dma_start(T.f2[half(x), o:o + b - a], T.f[half(x), a:b]).then_inc(S.df, 16)
+        f2 = op("g", [("cg", cnt["g"])], lambda: g.affine_select(T.f2[half(x), o:o + b - a], T.f[half(x), a:b], [[0, b - a]], A.is_ge, 0.0, 0, 0))
     zeros = [T.sw[:, NT:H]]
     if end:
         zeros.append(T.se[:, NT:H])
@@ -225,7 +251,14 @@ def rank_program(g, core, T, topo):
         need("p", *deps)
         fm, rows = (T.f, slice(0, 128)) if side is None else (T.f2, half(side))
         for q in range(16):
-            t = op("p", [], lambda: pe.matmul(out[:, a // 16:b // 16], fm[rows, 16 - q:144 - q], win[rows, H + a + q:H + b:16], q == 0, q == 15))
+            t = mm([], out[:, a // 16:b // 16], fm[rows, 16 - q:144 - q], win[rows, H + a + q:H + b:16], q == 0, q == 15)
+        return t
+
+    def first_list(out, a, scanned):
+        for q in range(1, 16, 2):
+            mm([zs, f], out[:, a // 16:a // 16 + LW], T.f[:, 16 - q:144 - q], T.d1[:, a + q:a + W:16], q == 1, False)
+        for q in range(0, 16, 2):
+            t = mm([scanned], out[:, a // 16:a // 16 + LW], T.f[:, FW + 16 - q:2 * FW - q], T.wa[:, H + a + q:H + a + W:16], False, q == 14)
         return t
 
     def emit(deps, out, src, add=None):
@@ -233,47 +266,56 @@ def rank_program(g, core, T, topo):
             return op("v", deps, lambda: v.tensor_copy(out, src))
         return op("v", deps, ts(out, src, add, None, A.add))
 
-    def jump(deps, out, o, win, z, lst, a, b, vc=None):
+    def jump(deps, out, o, win, z, lst, a, b, vc=None, inside=None):
         h = a + ((b - a) // 2 if vc is None else vc)
         e = o + 16 * (h - a)
-        t1 = op("v", deps, lambda: v.tensor_copy(out[:, o:e], win[:, 0:z].indirect(lst[:, a:h])))
         t2 = op("s", deps, lambda: s.activation(out[:, e:o + 16 * (b - a)], win[:, 0:z].indirect(lst[:, h:b]), CP))
+        cuts = [a, h] if inside is None else [a, a + inside[0], h]
+        for x, y in zip(cuts, cuts[1:]):
+            if x > a:
+                inside[1]()
+            t1 = op("v", deps, lambda: v.tensor_copy(out[:, o + 16 * (x - a):o + 16 * (y - a)], win[:, 0:z].indirect(lst[:, x:y])))
         return [t1, t2]
 
     full = P // 16
     head, tail = slice(0, LW), slice(LW, full)
     wins, bank = (T.wa, T.wb), (T.cvb, T.cva)
-    wrote = {(0, 0): [r[0], ia], (0, 1): [r[1]], (1, 0): [ib], (1, 1): []}
+    wrote = {(0, 0): [r[0]], (0, 1): [r[1]], (1, 0): [], (1, 1): []}
+    under = [[ia], ib]
     read = {x: [] for x in wrote}
     latest, turned, listed = [0, 0], [None, None], [None, None]
 
     def turn(x):
-        turned[x] = conv(wrote[latest[x], x] + [f], bank[x], wins[latest[x]], W * x, W * x + W)
+        turned[x] = conv(wrote[latest[x], x], bank[x], wins[latest[x]], W * x, W * x + W)
         read[latest[x], x].append(turned[x])
 
-    def gather(x, vc):
-        if turned[x]:
-            listed[x], turned[x] = emit([turned[x]], T.la[:, LW * x:LW * x + LW], bank[x][:, LW * x:LW * x + LW]), None
+    def move(x):
+        listed[x], turned[x] = emit([turned[x]], T.la[:, LW * x:LW * x + LW], bank[x][:, LW * x:LW * x + LW]), None
+
+    def gather(x, vc, inside=None):
         w = latest[x]
-        deps = [d for y in range(x + 1) for d in wrote[w, y]] + read[1 - w, x] + [listed[x]]
-        t = jump(deps, wins[1 - w], H + W * x, wins[w], H + W * x + W, T.la, LW * x, LW * x + LW, vc)
+        deps = [d for y in range(x + 1) for d in wrote[w, y]] + read[1 - w, x] + [listed[x]] + under[w]
+        t = jump(deps, wins[1 - w], H + W * x, wins[w], H + W * x + W, T.la, LW * x, LW * x + LW, vc, inside)
         for y in range(x + 1):
             read[w, y] += t
-        wrote[1 - w, x], read[1 - w, x], latest[x] = t + wrote[1 - w, x][-1:], [], 1 - w
+        wrote[1 - w, x], read[1 - w, x], latest[x] = t, [], 1 - w
         return t
 
-    turn(0)
-    turn(1)
-    for i, (x, turns) in enumerate(PLAN):
-        y = PLAN[i + 1][0] if i + 1 < len(PLAN) else 1
-        gather(x, VC if y != x and turned[y] else None)
+    for x in range(2):
+        turned[x] = first_list(bank[x], W * x, r[x])
+        read[0, x].append(turned[x])
+    move(0)
+    ib.append(columns("v", [], T.wb[:, H - B - K:H - B], 0, B - K))
+    for x, turns, vc, at in PLAN:
+        t = gather(x, vc, None if at is None or at == vc else (at, lambda: move(1 - x)))
+        if at == vc:
+            move(1 - x)
         if turns:
             turn(x)
 
-    t = gather(1, None)
     ps = {sh: T.cva, lg: T.cvc}
     so = [T.so[:, LW * x:LW * x + LW] for x in range(2)]
-    ctail = {sh: conv(t + [("df", 64)], ps[sh], wins[latest[1]], W, P, sh)}
+    ctail = {sh: conv(t + [f2], ps[sh], wins[latest[1]], W, P, sh)}
     if not end:
         ctail[lg] = conv([], ps[lg], wins[latest[1]], W, P, lg)
 
@@ -283,7 +325,7 @@ def rank_program(g, core, T, topo):
                                               srcs=[so[side]], dsts=[T.ll[:, LW * rank:LW * rank + LW] for _ in takers[side]])], local_sem=S.ls)
         return len(shared(rank))
 
-    t = gather(0, VC - 4)
+    t = gather(0, SHARE["last"])
     sent += send(sh)
     chead = conv(t, T.cvb, wins[latest[0]], 0, W)
     if end:

@@ -9,13 +9,15 @@ B = P // 3
 K = 256
 HT = NT // 2
 FW = 144
+RUN = 4
 RAW, CANCEL = 1, 3
 FOURS = 1.5 * 2 ** 25
 VC = 22
-PLAN = [(0, 1, 22, 14), (1, 0, 24, None), (1, 1, 22, 6), (0, 0, 24, None), (0, 1, 22, 6), (1, 0, 24, None), (1, 1, 22, 6),
-        (0, 0, 24, 24), (1, 1, 24, None), (0, 1, 24, 24), (1, 0, 24, 24)]
-SHARE = {"last": 16}
-LAG, LAST = {5: 0, 4: 3, 3: 1}, {5: 0.6, 4: 0.4, 3: 1.0}
+FOUR, FOURM, TWO, TWOM = "v12 s12 v12 s12", "v12 s12 move v12 s12", "v24 s24", "v24 s24 move"
+PLAN = [(0, "ab", 1, "v14 move v8 s26"), (1, "ab", 0, FOUR), (1, "bc", 1, FOURM), (0, "bc", 0, FOUR), (0, "ca", 1, FOURM),
+        (1, "ca", 0, FOUR), (1, "ab", 1, FOURM), (0, "ab", 0, TWOM), (1, "bc", 1, TWO), (0, "bc", 1, TWOM), (1, "ca", 0, TWOM),
+        (0, "ca", 0, "v18 s30")]
+LAG, LAST = {5: 0, 4: 2, 3: 1}, {5: 0.6, 4: 0.4, 3: 1.0}
 SCRATCH = {
     "lnb": ("sbuf", [128, C], "int32"), "dsr": ("sbuf", [128, HT + 8], "int32"),
     "sc": ("sbuf", [128, C], "float16"),
@@ -27,11 +29,11 @@ SCRATCH = {
     "ones": ("sbuf", [128, B], "bfloat16"), "cnt": ("sbuf", [128, B], "bfloat16"),
     "e0": ("sbuf", [128, 140], "bfloat16"), "qp": ("sbuf", [128, 140], "bfloat16"), "qn": ("sbuf", [128, 136], "bfloat16"),
     "gt": ("sbuf", [128, 128], "float16"), "dg": ("sbuf", [128, 128], "bfloat16"),
-    "fc": ("sbuf", [128, 9], "bfloat16"), "f": ("sbuf", [128, 2 * FW], "bfloat16"), "f2": ("sbuf", [128, FW], "bfloat16"),
-    "lt": ("sbuf", [128, NT], "bfloat16"),
+    "fc": ("sbuf", [128, 9 * RUN], "bfloat16"), "f": ("sbuf", [128, RUN * FW], "bfloat16"), "f2": ("sbuf", [128, FW], "bfloat16"),
+    "lt": ("sbuf", [128, NT], "bfloat16"), "i0": ("sbuf", [128, 1], "bfloat16"),
     "rd": ("sbuf", [128, HT + 16], "float16"), "z": ("sbuf", [128, NT], "bfloat16"),
     "d0": ("sbuf", [128, W], "bfloat16"), "d1": ("sbuf", [128, P], "bfloat16"),
-    "wa": ("sbuf", [128, H + P], "bfloat16"), "wb": ("sbuf", [128, H + P], "bfloat16"),
+    "wa": ("sbuf", [128, H + P], "bfloat16"), "wb": ("sbuf", [128, H + P], "bfloat16"), "wc": ("sbuf", [128, H + P], "bfloat16"),
     "la": ("sbuf", [128, P // 16], "uint16"),
     "so": ("sbuf", [128, 2 * LW], "uint16"), "ol": ("sbuf", [128, 2 * LW], "uint16"), "ll": ("sbuf", [128, N * LW], "uint16"),
     "sw": ("sbuf", [128, N * H], "bfloat16"), "se": ("sbuf", [128, H], "bfloat16"),
@@ -40,8 +42,9 @@ SCRATCH = {
     "car": ("psum", [128, 512], "float32"), "ini": ("psum", [128, 512], "float32"),
     "zpa": ("psum", [128, 32, 16], "float32"), "zpb": ("psum", [128, 32, 16], "float32"),
     "cva": ("psum", [128, 512], "float32"), "cvb": ("psum", [128, 512], "float32"), "cvc": ("psum", [128, 512], "float32"),
+    "cvd": ("psum", [128, 512], "float32"),
 }
-SEMAPHORES = ["cg", "cv", "cs", "cp", "dl", "dd", "dle", "lo", "lw", "st", "ls"]
+SEMAPHORES = ["cg", "cv", "cs", "cp", "dl", "dd", "dle", "lo", "st", "ls"] + ["lw%d" % k for k in range(N - 1)]
 SEMAPHORES += ["ar%d" % k for k in range(N)] + ["la%d" % k for k in range(N)]
 
 
@@ -142,16 +145,21 @@ def rank_program(g, core, T, topo):
     cb = op("v", [mb, co], ts(T.cb[:], T.cnt[:, K:K + 10:2], (H - 2 * B + K) / K, T.mb[:], A.add, A.mult))
     cl = op("v", [p6], ts(T.cl[:, 0:7], T.cnt[:, K:K + 7], T.p6[:], None, A.add))
     dg = op("v", [ma], ts(T.dg[:], T.xd[:, 0:128], 0.0, T.ma[:], A.is_equal, A.mult))
-    f0 = op("s", [ones], lambda: s.activation(T.f[:], T.ones[:, 0:2 * FW], CP, scale=0.0))
+    f0 = [op("s", [ones], lambda: s.activation(T.f[:, a:a + 2 * FW], T.ones[:, 0:2 * FW], CP, scale=0.0)) for a in range(0, RUN * FW, 2 * FW)][-1]
     p96 = op("s", [xd], lambda: s.activation(T.p96[:], T.xd[:, 0:1], CP, -1.0, float(P // 16)))
     mc = op("s", [p6], lambda: s.activation(T.mc[:], T.p6[:], F.Relu, (RAW + 1.5) * C / 2, -1.0))
     off = op("s", [p96], lambda: s.activation(T.off[:], T.p6[:], ID, T.p96[:], 16.0))
     qp = op("g", [e0], lambda: g.affine_select(T.qp[:], T.e0[:], [[1, 140]], A.not_equal, -1.0, 1 - CANCEL, -1))
-    f = op("g", [ones], lambda: g.affine_select(T.fc[:], T.ones[:, 0:9], [[-16, 9]], A.is_ge, 0.0, 16 - RAW, 1))
-    f = op("g", [f], lambda: g.affine_select(T.fc[:], T.fc[:], [[16, 9]], A.is_ge, 0.0, RAW + CANCEL + 1 - 16, -1))
-    op("g", [f, f0], lambda: g.affine_select(T.f[:, FW + 1:2 * FW:16], T.fc[:], [[16, 9]], A.is_ge, 0.0, RAW + 1 - 16, -1))
-    for a in (FW, 0):
-        f = op("g", [], lambda: g.affine_select(T.f[:, a:a + FW:16], T.fc[:], [[-16, 9]], A.not_equal, 0.0, 16 - (RAW + CANCEL - 1), 1))
+    def upto(deps, i, last):
+        return op("g", deps, lambda: g.affine_select(T.f[:, (FW + 1) * i:RUN * FW:16], T.fc[:, 9 * i:9 * RUN], [[0, RUN - i], [16, 9]],
+                                                     A.is_ge, 0.0, last - 16, -1))
+
+    f = op("g", [ones], lambda: g.affine_select(T.fc[:], T.ones[:, 0:9 * RUN], [[0, RUN], [-16, 9]], A.is_ge, 0.0, 16 - RAW, 1))
+    f = upto([f, f0], 0, RAW + CANCEL + 1)
+    for i in range(1, RUN - 1):
+        upto([], i, RAW + 1)
+    f = op("g", [f], lambda: g.affine_select(T.f[:, 0:RUN * FW:16], T.f[:, 0:RUN * FW:16], [[0, RUN], [-16, 9]], A.not_equal, 0.0, 16 - (RAW + CANCEL - 1), 1))
+    fl = upto([], RUN - 1, RAW + 1)
 
     def columns(q, deps, out, k, a=0):
         src = T.cnt[:, a:a + out.shape[1]]
@@ -187,6 +195,7 @@ def rank_program(g, core, T, topo):
     ini = mm([], T.ini[:, 0:1], T.qn[:, 0:128], T.rd[:, 0:1], True, True)
     zb = op("s", zz[:1], lambda: s.activation(T.z[:, HT:NT], T.zpb[:, 0:hc, :], CP))
     za = op("v", zz[1:], lambda: v.tensor_copy(T.z[:, 0:HT], T.zpa[:, 0:hc, :]))
+    ini = op("s", [ini], lambda: s.activation(T.i0[:], T.ini[:, 0:1], CP))
     dv = carry("v", [mc], B, W)
     dc = carry("s", [ones, mc], 0, B)
     columns("s", [], T.wa[:, H - B:H], 1)
@@ -197,7 +206,7 @@ def rank_program(g, core, T, topo):
     for a, o in ((0, 0), (W, K)):
         columns("v", [], T.wb[:, H - B + o:H - B + o + K], 1, o)
         r.append(op("v", r[-1:] if r else [zs, dc, dv, ini], lambda: v.tensor_tensor_scan(
-            T.wa[:, H + a:H + a + W], T.d0[:], T.d1[:, a:a + W], T.wa[:, H + a - 1:H + a] if a else T.ini[:, 0:1], A.mult, A.add)))
+            T.wa[:, H + a:H + a + W], T.d0[:], T.d1[:, a:a + W], T.wa[:, H + a - 1:H + a] if a else T.i0[:], A.mult, A.add)))
 
     def ids(rs):
         out = []
@@ -213,23 +222,17 @@ def rank_program(g, core, T, topo):
         es = [topo.engines(T.cores[src], T.cores[r]) for r in range(N) if r != src]
         return [e for e in es[0] if all(e in x for x in es)]
 
-    def letter_engines(src):
-        e = shared(src)
-        if src == 0:
-            return e, []
-        if src == N - 1:
-            return [], e
-        return e[:len(e) // 2], e[len(e) // 2:]
-
     for dst, side in own:
         sync.dma_start(dst, T.le[half(side), :]).then_inc(S.lo, 16)
     takers = [sorted(rs, key=lambda r: -gathers_left(rank, r)) for rs in (range(N - 1, rank, -1), range(rank))]
-    trs = [RemoteDMATransfer(dst_ids=ids(rs), dma_engine_mask=bits(letter_engines(rank)[side]), remote_sem=S["la%d" % rank],
-                             srcs=[T.dle[side]], dsts=[T.lel[rank] for _ in rs]) for side, rs in enumerate(takers) if rs]
-    g.wait_ge(S.dle, 16)
-    g.remote_dma_fused(trs, local_sem=S.ls)
-    sent = sum(len(e) for e in letter_engines(rank))
+    need("g", ("dle", 16))
+    sent = 0
+    for side in ([sh] if end else [sh, lg]):
+        g.remote_dma_fused([RemoteDMATransfer(dst_ids=ids(takers[side]), dma_engine_mask=bits(shared(rank)), remote_sem=S["la%d" % rank],
+                                              srcs=[T.dle[side]], dsts=[T.lel[rank] for _ in takers[side]])], local_sem=S.ls)
+        sent += len(shared(rank))
 
+    ic = [op("g", [ia], lambda: g.affine_select(T.wc[:, 0:H], T.wa[:, 0:H], [[0, H]], A.is_ge, 0.0, 0, 0))]
     for x, o, a, b in ((0, 0, 0, 80), (0, 80, 16, 80), (1, 0, 64, 144), (1, 80, 80, 144)):
         f2 = op("g", [("cg", cnt["g"])], lambda: g.affine_select(T.f2[half(x), o:o + b - a], T.f[half(x), a:b], [[0, b - a]], A.is_ge, 0.0, 0, 0))
     zeros = [T.sw[:, NT:H]]
@@ -240,12 +243,12 @@ def rank_program(g, core, T, topo):
         zeros += [letters(sh, k) for k in range(n + 1) if k not in used]
     for x in zeros:
         z0 = op("g", [("cg", cnt["g"])], lambda: g.iota(x, [[0, x.shape[1]]], 0, 0, **flag))
-    landed = 0
-    for (side, k), src in sorted(source.items(), key=lambda x: call_of(x[1], rank)):
-        need("y", ("la%d" % src, len(letter_engines(src)[side])))
+    landed = [0] * n
+    for (side, k), src in sorted(source.items(), key=lambda x: slot(*x[0])):
+        need("y", ("la%d" % src, len(shared(src))))
         for x in (range(2) if end else [side]):
-            sync.dma_start(letters(x, slot(side, k)), T.lel[src]).then_inc(S.lw, 16)
-            landed += 16
+            sync.dma_start(letters(x, slot(side, k)), T.lel[src]).then_inc(S["lw%d" % slot(side, k)], 16)
+            landed[slot(side, k)] += 16
 
     def conv(deps, out, win, a, b, side=None):
         need("p", *deps)
@@ -255,10 +258,9 @@ def rank_program(g, core, T, topo):
         return t
 
     def first_list(out, a, scanned):
-        for q in range(1, 16, 2):
-            mm([zs, f], out[:, a // 16:a // 16 + LW], T.f[:, 16 - q:144 - q], T.d1[:, a + q:a + W:16], q == 1, False)
-        for q in range(0, 16, 2):
-            t = mm([scanned], out[:, a // 16:a // 16 + LW], T.f[:, FW + 16 - q:2 * FW - q], T.wa[:, H + a + q:H + a + W:16], False, q == 14)
+        for q in sorted(range(16), key=lambda q: q % RUN == 0):
+            o, src = FW * (RUN - 1 - q % RUN), T.d1[:, a + q:a + W:16] if q % RUN else T.wa[:, H + a + q:H + a + W:16]
+            t = mm([zs, f] if q % RUN else [scanned, fl], out[:, a // 16:a // 16 + LW], T.f[:, o + 16 - q:o + FW - q], src, q == 1, q == 16 - RUN)
         return t
 
     def emit(deps, out, src, add=None):
@@ -266,58 +268,65 @@ def rank_program(g, core, T, topo):
             return op("v", deps, lambda: v.tensor_copy(out, src))
         return op("v", deps, ts(out, src, add, None, A.add))
 
-    def jump(deps, out, o, win, z, lst, a, b, vc=None, inside=None):
+    def jump(deps, out, o, win, z, lst, a, b, vc=None):
         h = a + ((b - a) // 2 if vc is None else vc)
         e = o + 16 * (h - a)
+        t1 = op("v", deps, lambda: v.tensor_copy(out[:, o:e], win[:, 0:z].indirect(lst[:, a:h])))
         t2 = op("s", deps, lambda: s.activation(out[:, e:o + 16 * (b - a)], win[:, 0:z].indirect(lst[:, h:b]), CP))
-        cuts = [a, h] if inside is None else [a, a + inside[0], h]
-        for x, y in zip(cuts, cuts[1:]):
-            if x > a:
-                inside[1]()
-            t1 = op("v", deps, lambda: v.tensor_copy(out[:, o + 16 * (x - a):o + 16 * (y - a)], win[:, 0:z].indirect(lst[:, x:y])))
         return [t1, t2]
 
     full = P // 16
     head, tail = slice(0, LW), slice(LW, full)
-    wins, bank = (T.wa, T.wb), (T.cvb, T.cva)
-    wrote = {(0, 0): [r[0]], (0, 1): [r[1]], (1, 0): [], (1, 1): []}
-    under = [[ia], ib]
-    read = {x: [] for x in wrote}
-    latest, turned, listed = [0, 0], [None, None], [None, None]
+    wins, bank = {"a": T.wa, "b": T.wb, "c": T.wc}, (T.cvb, T.cva)
+    wrote = {"a": [(0, W, r[0]), (W, P, r[1])], "b": [], "c": []}
+    read = {w: [] for w in wins}
+    under = {"a": [ia], "b": ib, "c": ic}
+    turned, listed = [None, None], [None, None]
 
-    def turn(x):
-        turned[x] = conv(wrote[latest[x], x], bank[x], wins[latest[x]], W * x, W * x + W)
-        read[latest[x], x].append(turned[x])
+    def met(calls, lo, hi):
+        return [t for a, b, t in calls if a < hi and lo < b]
+
+    def turn(out, w, x, side=None):
+        t = conv(met(wrote[w], W * x, W * x + W), out, wins[w], W * x, W * x + W, side)
+        read[w].append((W * x, W * x + W, t))
+        return t
 
     def move(x):
-        listed[x], turned[x] = emit([turned[x]], T.la[:, LW * x:LW * x + LW], bank[x][:, LW * x:LW * x + LW]), None
+        listed[x] = emit([turned[x]], T.la[:, LW * x:LW * x + LW], bank[x][:, LW * x:LW * x + LW])
 
-    def gather(x, vc, inside=None):
-        w = latest[x]
-        deps = [d for y in range(x + 1) for d in wrote[w, y]] + read[1 - w, x] + [listed[x]] + under[w]
-        t = jump(deps, wins[1 - w], H + W * x, wins[w], H + W * x + W, T.la, LW * x, LW * x + LW, vc, inside)
-        for y in range(x + 1):
-            read[w, y] += t
-        wrote[1 - w, x], read[1 - w, x], latest[x] = t, [], 1 - w
-        return t
+    def gather(x, way, calls):
+        src, dst = way
+        a, done = LW * x, []
+        for call in calls.split():
+            if call == "move":
+                move(1 - x)
+                continue
+            q, b = call[0], a + int(call[1:])
+            out, win = wins[dst][:, H + 16 * a:H + 16 * b], wins[src][:, 0:H + 16 * b].indirect(T.la[:, a:b])
+            deps = met(wrote[src], 0, 16 * b) + under[src] + met(read[dst] + wrote[dst], 16 * a, 16 * b) + [listed[x]]
+            t = op(q, deps, (lambda: v.tensor_copy(out, win)) if q == "v" else lambda: s.activation(out, win, CP))
+            done.append((16 * a, 16 * b, t))
+            a = b
+        read[src] += [(0, b, t) for a, b, t in done]
+        wrote[dst] += done
 
     for x in range(2):
         turned[x] = first_list(bank[x], W * x, r[x])
-        read[0, x].append(turned[x])
+        read["a"].append((W * x, W * x + W, turned[x]))
     move(0)
     ib.append(columns("v", [], T.wb[:, H - B - K:H - B], 0, B - K))
-    for x, turns, vc, at in PLAN:
-        t = gather(x, vc, None if at is None or at == vc else (at, lambda: move(1 - x)))
-        if at == vc:
-            move(1 - x)
+    for x, way, turns, calls in PLAN[:-1]:
+        gather(x, way, calls)
         if turns:
-            turn(x)
+            turned[x] = turn(bank[x], way[1], x)
 
     ps = {sh: T.cva, lg: T.cvc}
     so = [T.so[:, LW * x:LW * x + LW] for x in range(2)]
-    ctail = {sh: conv(t + [f2], ps[sh], wins[latest[1]], W, P, sh)}
+    wt, wh = PLAN[-2][1][1], PLAN[-1][1][1]
+    need("p", f2)
+    ctail = {sh: turn(ps[sh], wt, 1, sh)}
     if not end:
-        ctail[lg] = conv([], ps[lg], wins[latest[1]], W, P, lg)
+        ctail[lg] = turn(ps[lg], wt, 1, lg)
 
     def send(side):
         need("g", emit([ctail[side]], so[side], ps[side][:, tail], float(H * piece(rank, side))))
@@ -325,12 +334,14 @@ def rank_program(g, core, T, topo):
                                               srcs=[so[side]], dsts=[T.ll[:, LW * rank:LW * rank + LW] for _ in takers[side]])], local_sem=S.ls)
         return len(shared(rank))
 
-    t = gather(0, SHARE["last"])
+    gather(0, PLAN[-1][1], PLAN[-1][3])
     sent += send(sh)
-    chead = conv(t, T.cvb, wins[latest[0]], 0, W)
     if end:
-        ctail[lg] = conv([], ps[lg], wins[latest[1]], W, P, lg)
+        first = [turn(T.cvb, wh, 0, sh), ctail[sh]]
+        chead = turn(T.cvd, wh, 0, lg)
+        ctail[lg] = turn(ps[lg], wt, 1, lg)
     else:
+        chead = turn(T.cvb, wh, 0)
         sent += send(lg)
 
     stored = [0]
@@ -341,13 +352,20 @@ def rank_program(g, core, T, topo):
         stored[0] += 16
 
     if end:
-        emit([], T.ol[half(lg), head], ps[sh][half(lg), tail])
-        e = emit([chead], T.ol[half(sh), head], T.cvb[half(sh), head])
-        t = jump([e, z0, ("lo", 16 * len(own))], T.yo, W, T.se, H, T.ol, 0, LW, VC - 2)
-        store("y", t + [("ls", sent)], half(sh), 0, T.yo[half(sh), W:P])
-        store("y", t, half(sh), W, T.yo[half(lg), W:P])
-        emit([], T.ol[half(lg), tail], T.cvb[half(lg), head], float(H * n))
-        mine = emit([ctail[lg]], T.ol[half(sh), tail], ps[lg][half(sh), tail], float(H * n))
+        hw = LW // 2
+
+        def split(x):
+            src = ps[sh] if x else T.cvb
+            return [emit([first[x]], T.ol[half(u), hw * x:hw * x + hw], src[half(u), LW * x + hw * u:LW * x + hw * u + hw]) for u in range(2)][-1]
+
+        def unpack(x, listed, a, b, vc=None):
+            o = W + 16 * hw * x
+            t = jump([listed, z0, ("lo", 16 * len(own))], T.yo, o + 16 * a, T.se, H, T.ol, hw * x + a, hw * x + b, vc)
+            for u in (range(2) if b == hw else []):
+                store("y", t + [("ls", sent)], half(sh), W * x + 16 * hw * u, T.yo[half(u), o:o + 16 * hw])
+
+        unpack(1, split(1), 0, hw, 16)
+        listed = split(0)
     else:
         if spare == 1:
             emit([chead], T.ol[half(lg), head], T.cvb[half(lg), head], float(H * n))
@@ -371,14 +389,19 @@ def rank_program(g, core, T, topo):
             return [emit(deps + [arrived(src)], dst, T.ll[half(sh), LW * src:LW * src + LW], float(H * (slot(sh, j) - j)))]
         return [emit(deps, dst, T.cvb[half(sh), head] if j == m else ps[sh][half(sh), tail], float(H * slot(sh, m)))]
 
-    ready = [z0, ("lw", landed), ("lo", 16 * len(own))] + short(0)
+    ready = [z0, ("lo", 16 * len(own))] + short(0)
     for k in range(n):
         src = source[lg, k]
         more = not end and lagged <= k + 1 < n
-        ready = jump(ready + [arrived(src)], T.sw, H * (k + 1) + NT, T.sw, H * (k + 1), T.ll, LW * src, LW * src + LW, VC if more else None)
+        ready = jump(ready + [("lw%d" % k, landed[k]), arrived(src)], T.sw, H * (k + 1) + NT, T.sw, H * (k + 1), T.ll, LW * src, LW * src + LW, VC if more else None)
         if not end and k >= lagged + m:
             store("y", ready, half(sh), W * (k - lagged - m), T.sw[half(sh), H * (k + 1) + NT:H * (k + 2)])
         ready = ready + short(k + 1)
+        if end and k < 3:
+            unpack(0, listed, hw // 3 * k, hw // 3 * (k + 1))
+        if end and k == 3:
+            emit([chead], T.ol[half(lg), tail], T.cvd[half(lg), head], float(H * n))
+            mine = emit([ctail[lg]], T.ol[half(sh), tail], ps[lg][half(sh), tail], float(H * n))
 
     ready.append(mine)
     if end:
@@ -388,8 +411,7 @@ def rank_program(g, core, T, topo):
     elif spare:
         t = jump(ready, T.yo, 0, T.sw, H * (n + 1), T.ol, 0, LW)
         store("y", t, half(lg), 0, T.yo[half(lg), 0:W])
-        if spare == 1:
-            store("y", t, half(sh), W, T.yo[half(sh), 0:W])
+        store("y", t, half(sh), W, T.yo[half(sh), 0:W])
         t = jump(ready, T.yo, W, T.sw, H * (n + 1), T.so, LW * lg, LW * lg + LW)
         store("y", t, half(lg), W, T.yo[half(lg), W:P])
     else:

from concourse.bass import DstId, RemoteDMATransfer
from concourse.mybir import AluOpType, ActivationFunctionType

N, P, NT, W = 6, 1536, 192, 768
H = NT + W
C = NT // 16
LW = W // 16
B = P // 3
K = 256
HT = NT // 2
FW = 144
RUN = 4
RAW, CANCEL = 1, 3
FOURS = 1.5 * 2 ** 25
VC = 22
FOUR, FOURM, TWO, TWOM = "v12 s12 v12 s12", "v12 s12 move v12 s12", "v24 s24", "v24 s24 move"
PLAN = [(0, "ab", 1, "v14 move v8 s26"), (1, "ab", 0, FOUR), (1, "bc", 1, FOURM), (0, "bc", 0, FOUR), (0, "ca", 1, FOURM),
        (1, "ca", 0, FOUR), (1, "ab", 1, FOURM), (0, "ab", 0, TWOM), (1, "bc", 1, TWO), (0, "bc", 1, TWOM), (1, "ca", 0, TWOM),
        (0, "ca", 0, "v18 s30")]
LAG, LAST = {5: 0, 4: 2, 3: 1}, {5: 0.6, 4: 0.4, 3: 1.0}
SCRATCH = {
    "lnb": ("sbuf", [128, C], "int32"), "dsr": ("sbuf", [128, HT + 8], "int32"),
    "sc": ("sbuf", [128, C], "float16"),
    "lasts": ("sbuf", [128, C], "uint16"), "cl": ("sbuf", [128, 8], "uint16"),
    "pi": ("sbuf", [128, 1], "int32"), "pj": ("sbuf", [128, 1], "int32"), "xd": ("sbuf", [128, 140], "bfloat16"),
    "p2": ("sbuf", [128, 1], "int32"), "p6": ("sbuf", [128, 1], "float32"), "mc": ("sbuf", [128, 1], "float32"),
    "ma": ("sbuf", [128, 1], "float32"), "mb": ("sbuf", [128, 1], "float32"), "mr": ("sbuf", [128, 1], "float32"),
    "p96": ("sbuf", [128, 1], "float32"), "off": ("sbuf", [128, 1], "float32"), "cb": ("sbuf", [128, 5], "float32"),
    "ones": ("sbuf", [128, B], "bfloat16"), "cnt": ("sbuf", [128, B], "bfloat16"),
    "e0": ("sbuf", [128, 140], "bfloat16"), "qp": ("sbuf", [128, 140], "bfloat16"), "qn": ("sbuf", [128, 136], "bfloat16"),
    "gt": ("sbuf", [128, 128], "float16"), "dg": ("sbuf", [128, 128], "bfloat16"),
    "fc": ("sbuf", [128, 9 * RUN], "bfloat16"), "f": ("sbuf", [128, RUN * FW], "bfloat16"), "f2": ("sbuf", [128, FW], "bfloat16"),
    "lt": ("sbuf", [128, NT], "bfloat16"), "i0": ("sbuf", [128, 1], "bfloat16"),
    "rd": ("sbuf", [128, HT + 16], "float16"), "z": ("sbuf", [128, NT], "bfloat16"),
    "d0": ("sbuf", [128, W], "bfloat16"), "d1": ("sbuf", [128, P], "bfloat16"),
    "wa": ("sbuf", [128, H + P], "bfloat16"), "wb": ("sbuf", [128, H + P], "bfloat16"), "wc": ("sbuf", [128, H + P], "bfloat16"),
    "la": ("sbuf", [128, P // 16], "uint16"),
    "so": ("sbuf", [128, 2 * LW], "uint16"), "ol": ("sbuf", [128, 2 * LW], "uint16"), "ll": ("sbuf", [128, N * LW], "uint16"),
    "sw": ("sbuf", [128, N * H], "bfloat16"), "se": ("sbuf", [128, H], "bfloat16"),
    "yo": ("sbuf", [128, P], "bfloat16"),
    "dle": ("dram", [2, 128, NT // 2], "bfloat16"), "lel": ("dram", [N, 128, NT // 2], "bfloat16"),
    "car": ("psum", [128, 512], "float32"), "ini": ("psum", [128, 512], "float32"),
    "zpa": ("psum", [128, 32, 16], "float32"), "zpb": ("psum", [128, 32, 16], "float32"),
    "cva": ("psum", [128, 512], "float32"), "cvb": ("psum", [128, 512], "float32"), "cvc": ("psum", [128, 512], "float32"),
    "cvd": ("psum", [128, 512], "float32"),
}
SEMAPHORES = ["cg", "cv", "cs", "cp", "dl", "dd", "dle", "lo", "st", "ls"] + ["lw%d" % k for k in range(N - 1)]
SEMAPHORES += ["ar%d" % k for k in range(N)] + ["la%d" % k for k in range(N)]


def piece(r, side):
    return N - 1 - r if side else r


def long_side(r):
    return 0 if piece(r, 0) > piece(r, 1) else 1


def lag(r):
    return LAG[piece(r, long_side(r))]


def call_of(src, dst):
    side = 0 if src < dst else 1
    return piece(src, side) + (lag(dst) if side != long_side(dst) else 0)


def gathers_left(src, dst):
    n = piece(dst, long_side(dst))
    return n + (1 if n == N - 1 else 2) - call_of(src, dst) + LAST[n]


def rank_program(g, core, T, topo):
    rank = T.rank_of(core)
    if rank is None:
        return
    A, F = AluOpType, ActivationFunctionType
    CP, ID = F.Copy, F.Identity
    v, s, pe, sync, S = g.vector, g.scalar, g.tensor, g.sync, T.sem
    queue = {"g": g, "v": v, "s": s, "p": pe, "y": sync}
    cnt = {"g": 0, "v": 0, "s": 0, "p": 0}
    seen = {}

    def need(q, *deps):
        for sem, val in deps:
            if seen.get((q, sem), 0) < val:
                queue[q].wait_ge(S[sem], val)
                seen[(q, sem)] = val

    def op(q, deps, ins):
        need(q, *deps)
        cnt[q] += 1
        ins().then_inc(S["c" + q], 1)
        return ("c" + q, cnt[q])

    def ts(out, in0, s1, s2, *ops):
        return lambda: v.tensor_scalar(out, in0, s1, s2, *ops)

    def mm(deps, out, lhs, rhs, first, last):
        return op("p", deps, lambda: pe.matmul(out, lhs, rhs, first, last))

    def half(side):
        return slice(64 * side, 64 * side + 64)

    lg = long_side(rank)
    sh = 1 - lg
    n, m = piece(rank, lg), piece(rank, sh)
    end = m == 0
    lagged = lag(rank)
    spare = n - m - lagged
    source = {(side, k): piece(k, side) for side in range(2) for k in range(piece(rank, side))}

    def slot(side, k):
        return k + lagged if side == sh and k > 0 else k

    def letters(side, k):
        return T.sw[half(side), H * k:H * k + NT]

    sync.dma_start(T.lnb[:], T.ln[:]).then_inc(S.dl, 16)
    dz = op("v", [], lambda: v.memset(T.dsr[:], 0))
    need("y", dz)
    need("s", dz)
    s.dma_start(T.dsr[RAW:128:8, 0:HT], T.ds[:]).then_inc(S.dd, 16)
    sync.dma_start(T.dsr[RAW + 1:128:8, 0:HT], T.ds[:]).then_inc(S.dd, 16)
    sync.dma_start(T.dle[:], T.le[:]).then_inc(S.dle, 16)
    if end:
        own = [(letters(x, n), lg) for x in range(2)] + [(T.se[half(x), 0:NT], sh) for x in range(2)]
    else:
        own = [(letters(x, slot(x, piece(rank, x))), x) for x in range(2)]

    flag = {"allow_small_or_imprecise_dtypes": True}
    pi = op("g", [], lambda: g.iota(T.pi[:], [[1, 1]], 0, 1))
    xd = op("g", [], lambda: g.iota(T.xd[:], [[1, 140]], 0, -1, **flag))
    lt = op("g", [], lambda: g.iota(T.lt[:], [[1, C], [C, 16]], 0, 0, **flag))
    ones = op("v", [], lambda: v.memset(T.ones[:], 1.0))
    pj = op("v", [pi], ts(T.pj[:], T.pi[:], 15, None, A.bitwise_and))
    p2 = op("v", [], ts(T.p2[:], T.pi[:], RAW + 1, None, A.bitwise_and))
    co = op("v", [ones], lambda: v.tensor_tensor_scan(T.cnt[:], T.ones[:], T.ones[:], -K - 1.0, A.add, A.mult))
    e0 = op("v", [xd], ts(T.e0[:], T.xd[:], float(CANCEL), None, A.is_equal))
    mb = op("v", [pj], ts(T.mb[:], T.pj[:], float(RAW + CANCEL + 1), float(K), A.is_equal, A.mult))
    p6 = op("v", [], ts(T.p6[:], T.pj[:], float(C // 2), None, A.mult))
    ma = op("v", [], ts(T.ma[:], T.pj[:], float(RAW + CANCEL), None, A.is_equal))
    mr = op("v", [p2], ts(T.mr[:], T.p2[:], FOURS / (RAW + 1), None, A.mult))
    gt = op("v", [], ts(T.gt[:], T.xd[:, 0:128], 0.0, None, A.is_gt))
    cb = op("v", [mb, co], ts(T.cb[:], T.cnt[:, K:K + 10:2], (H - 2 * B + K) / K, T.mb[:], A.add, A.mult))
    cl = op("v", [p6], ts(T.cl[:, 0:7], T.cnt[:, K:K + 7], T.p6[:], None, A.add))
    dg = op("v", [ma], ts(T.dg[:], T.xd[:, 0:128], 0.0, T.ma[:], A.is_equal, A.mult))
    f0 = [op("s", [ones], lambda: s.activation(T.f[:, a:a + 2 * FW], T.ones[:, 0:2 * FW], CP, scale=0.0)) for a in range(0, RUN * FW, 2 * FW)][-1]
    p96 = op("s", [xd], lambda: s.activation(T.p96[:], T.xd[:, 0:1], CP, -1.0, float(P // 16)))
    mc = op("s", [p6], lambda: s.activation(T.mc[:], T.p6[:], F.Relu, (RAW + 1.5) * C / 2, -1.0))
    off = op("s", [p96], lambda: s.activation(T.off[:], T.p6[:], ID, T.p96[:], 16.0))
    qp = op("g", [e0], lambda: g.affine_select(T.qp[:], T.e0[:], [[1, 140]], A.not_equal, -1.0, 1 - CANCEL, -1))
    def upto(deps, i, last):
        return op("g", deps, lambda: g.affine_select(T.f[:, (FW + 1) * i:RUN * FW:16], T.fc[:, 9 * i:9 * RUN], [[0, RUN - i], [16, 9]],
                                                     A.is_ge, 0.0, last - 16, -1))

    f = op("g", [ones], lambda: g.affine_select(T.fc[:], T.ones[:, 0:9 * RUN], [[0, RUN], [-16, 9]], A.is_ge, 0.0, 16 - RAW, 1))
    f = upto([f, f0], 0, RAW + CANCEL + 1)
    for i in range(1, RUN - 1):
        upto([], i, RAW + 1)
    f = op("g", [f], lambda: g.affine_select(T.f[:, 0:RUN * FW:16], T.f[:, 0:RUN * FW:16], [[0, RUN], [-16, 9]], A.not_equal, 0.0, 16 - (RAW + CANCEL - 1), 1))
    fl = upto([], RUN - 1, RAW + 1)

    def columns(q, deps, out, k, a=0):
        src = T.cnt[:, a:a + out.shape[1]]
        if q == "v":
            return op(q, deps, ts(out, src, T.ma[:], T.cb[:, k:k + 1], A.mult, A.add))
        return op(q, deps, lambda: s.activation(out, src, ID, T.cb[:, k:k + 1], T.ma[:]))

    def carry(q, deps, a, b):
        if q == "v":
            return op(q, deps, ts(T.d0[:, a:b], T.ones[:, 0:b - a], T.mc[:], 0.0, A.mult, A.is_gt))
        return op(q, deps, lambda: s.activation(T.d0[:, a:b], T.ones[:, 0:b - a], F.Sign, scale=T.mc[:]))

    zp = (T.zpa, T.zpb)
    columns("s", [co, ma, cb], T.d1[:, 0:B], 2)
    x1 = columns("s", [], T.d1[:, B:2 * B], 3)
    for u in range(2):
        mm([dg, lt], zp[u][:, 0:C // 2, :], T.dg[:], T.lt[:, HT * u:HT * u + HT], True, False)
    sc = op("v", [("dl", 16)], lambda: v.tensor_tensor_scan(T.sc[:], T.lnb[:], T.ones[:, 0:C], 0.0, A.add, A.add))
    car = mm([gt, sc], T.car[:, 0:1], T.gt[:], T.sc[:, C - 1:C], True, True)
    rd = op("v", [cl, mr, ("dd", 32)], ts(T.rd[:], T.dsr[:].indirect(T.cl[:, 0:7]), T.mr[:], T.mr[:], A.add, A.subtract))
    qn = op("v", [qp], lambda: v.tensor_tensor(T.qn[:], T.qp[:, 0:136], T.qp[:, CANCEL:CANCEL + 136], A.subtract))
    x0 = columns("v", [cb], T.d1[:, 2 * B:P], 4)
    lasts = op("v", [car, sc, off], ts(T.lasts[:], T.sc[:], T.car[:, 0:1], T.off[:], A.add, A.add))
    hc, zz = C // 2, []
    for x in range(2):
        for u in range(2):
            mm([qp, rd], zp[x][:, 0:hc, 8 * u:8 * u + 8], T.qp[:, CANCEL + 8 * u:CANCEL + 8 * u + 128], T.rd[:, x:HT:2], False, False)
    mm([qn], T.zpb[:, hc - 1, 7:8], T.qn[:, 8:136], T.rd[:, 0:1], False, False)
    for x in (1, 0):
        for u in range(2):
            t = mm([], zp[x][:, 0:hc, 8 * u:8 * u + 8], T.qn[:, 8 * u:8 * u + 128], T.rd[:, 16 + x:HT + 16:2], False, u == 1)
        zz.append(t)
    ini = mm([], T.ini[:, 0:1], T.qn[:, 0:128], T.rd[:, 0:1], True, True)
    zb = op("s", zz[:1], lambda: s.activation(T.z[:, HT:NT], T.zpb[:, 0:hc, :], CP))
    za = op("v", zz[1:], lambda: v.tensor_copy(T.z[:, 0:HT], T.zpa[:, 0:hc, :]))
    ini = op("s", [ini], lambda: s.activation(T.i0[:], T.ini[:, 0:1], CP))
    dv = carry("v", [mc], B, W)
    dc = carry("s", [ones, mc], 0, B)
    columns("s", [], T.wa[:, H - B:H], 1)
    ia = columns("s", [], T.wa[:, 0:H - B], 0, 2 * B - H)
    ib = [columns("s", [], T.wb[:, 0:H - B - K], 0, 2 * B - H)]
    zs = op("v", [za, zb, lasts, x0, x1], lambda: v.tensor_copy(T.d1[:, 0:P].indirect(T.lasts[:, 0:C]), T.z[:]))
    r = []
    for a, o in ((0, 0), (W, K)):
        columns("v", [], T.wb[:, H - B + o:H - B + o + K], 1, o)
        r.append(op("v", r[-1:] if r else [zs, dc, dv, ini], lambda: v.tensor_tensor_scan(
            T.wa[:, H + a:H + a + W], T.d0[:], T.d1[:, a:a + W], T.wa[:, H + a - 1:H + a] if a else T.i0[:], A.mult, A.add)))

    def ids(rs):
        out = []
        for r in rs:
            a = topo.addr(T.cores[r])
            out.append(DstId(rid=a[0], pnc=a[1]))
        return out

    def bits(engines):
        return sum(1 << e for e in engines)

    def shared(src):
        es = [topo.engines(T.cores[src], T.cores[r]) for r in range(N) if r != src]
        return [e for e in es[0] if all(e in x for x in es)]

    for dst, side in own:
        sync.dma_start(dst, T.le[half(side), :]).then_inc(S.lo, 16)
    takers = [sorted(rs, key=lambda r: -gathers_left(rank, r)) for rs in (range(N - 1, rank, -1), range(rank))]
    need("g", ("dle", 16))
    sent = 0
    for side in ([sh] if end else [sh, lg]):
        g.remote_dma_fused([RemoteDMATransfer(dst_ids=ids(takers[side]), dma_engine_mask=bits(shared(rank)), remote_sem=S["la%d" % rank],
                                              srcs=[T.dle[side]], dsts=[T.lel[rank] for _ in takers[side]])], local_sem=S.ls)
        sent += len(shared(rank))

    ic = [op("g", [ia], lambda: g.affine_select(T.wc[:, 0:H], T.wa[:, 0:H], [[0, H]], A.is_ge, 0.0, 0, 0))]
    for x, o, a, b in ((0, 0, 0, 80), (0, 80, 16, 80), (1, 0, 64, 144), (1, 80, 80, 144)):
        f2 = op("g", [("cg", cnt["g"])], lambda: g.affine_select(T.f2[half(x), o:o + b - a], T.f[half(x), a:b], [[0, b - a]], A.is_ge, 0.0, 0, 0))
    zeros = [T.sw[:, NT:H]]
    if end:
        zeros.append(T.se[:, NT:H])
    else:
        used = [slot(sh, k) for k in range(m + 1)]
        zeros += [letters(sh, k) for k in range(n + 1) if k not in used]
    for x in zeros:
        z0 = op("g", [("cg", cnt["g"])], lambda: g.iota(x, [[0, x.shape[1]]], 0, 0, **flag))
    landed = [0] * n
    for (side, k), src in sorted(source.items(), key=lambda x: slot(*x[0])):
        need("y", ("la%d" % src, len(shared(src))))
        for x in (range(2) if end else [side]):
            sync.dma_start(letters(x, slot(side, k)), T.lel[src]).then_inc(S["lw%d" % slot(side, k)], 16)
            landed[slot(side, k)] += 16

    def conv(deps, out, win, a, b, side=None):
        need("p", *deps)
        fm, rows = (T.f, slice(0, 128)) if side is None else (T.f2, half(side))
        for q in range(16):
            t = mm([], out[:, a // 16:b // 16], fm[rows, 16 - q:144 - q], win[rows, H + a + q:H + b:16], q == 0, q == 15)
        return t

    def first_list(out, a, scanned):
        for q in sorted(range(16), key=lambda q: q % RUN == 0):
            o, src = FW * (RUN - 1 - q % RUN), T.d1[:, a + q:a + W:16] if q % RUN else T.wa[:, H + a + q:H + a + W:16]
            t = mm([zs, f] if q % RUN else [scanned, fl], out[:, a // 16:a // 16 + LW], T.f[:, o + 16 - q:o + FW - q], src, q == 1, q == 16 - RUN)
        return t

    def emit(deps, out, src, add=None):
        if add is None:
            return op("v", deps, lambda: v.tensor_copy(out, src))
        return op("v", deps, ts(out, src, add, None, A.add))

    def jump(deps, out, o, win, z, lst, a, b, vc=None):
        h = a + ((b - a) // 2 if vc is None else vc)
        e = o + 16 * (h - a)
        t1 = op("v", deps, lambda: v.tensor_copy(out[:, o:e], win[:, 0:z].indirect(lst[:, a:h])))
        t2 = op("s", deps, lambda: s.activation(out[:, e:o + 16 * (b - a)], win[:, 0:z].indirect(lst[:, h:b]), CP))
        return [t1, t2]

    full = P // 16
    head, tail = slice(0, LW), slice(LW, full)
    wins, bank = {"a": T.wa, "b": T.wb, "c": T.wc}, (T.cvb, T.cva)
    wrote = {"a": [(0, W, r[0]), (W, P, r[1])], "b": [], "c": []}
    read = {w: [] for w in wins}
    under = {"a": [ia], "b": ib, "c": ic}
    turned, listed = [None, None], [None, None]

    def met(calls, lo, hi):
        return [t for a, b, t in calls if a < hi and lo < b]

    def turn(out, w, x, side=None):
        t = conv(met(wrote[w], W * x, W * x + W), out, wins[w], W * x, W * x + W, side)
        read[w].append((W * x, W * x + W, t))
        return t

    def move(x):
        listed[x] = emit([turned[x]], T.la[:, LW * x:LW * x + LW], bank[x][:, LW * x:LW * x + LW])

    def gather(x, way, calls):
        src, dst = way
        a, done = LW * x, []
        for call in calls.split():
            if call == "move":
                move(1 - x)
                continue
            q, b = call[0], a + int(call[1:])
            out, win = wins[dst][:, H + 16 * a:H + 16 * b], wins[src][:, 0:H + 16 * b].indirect(T.la[:, a:b])
            deps = met(wrote[src], 0, 16 * b) + under[src] + met(read[dst] + wrote[dst], 16 * a, 16 * b) + [listed[x]]
            t = op(q, deps, (lambda: v.tensor_copy(out, win)) if q == "v" else lambda: s.activation(out, win, CP))
            done.append((16 * a, 16 * b, t))
            a = b
        read[src] += [(0, b, t) for a, b, t in done]
        wrote[dst] += done

    for x in range(2):
        turned[x] = first_list(bank[x], W * x, r[x])
        read["a"].append((W * x, W * x + W, turned[x]))
    move(0)
    ib.append(columns("v", [], T.wb[:, H - B - K:H - B], 0, B - K))
    for x, way, turns, calls in PLAN[:-1]:
        gather(x, way, calls)
        if turns:
            turned[x] = turn(bank[x], way[1], x)

    ps = {sh: T.cva, lg: T.cvc}
    so = [T.so[:, LW * x:LW * x + LW] for x in range(2)]
    wt, wh = PLAN[-2][1][1], PLAN[-1][1][1]
    need("p", f2)
    ctail = {sh: turn(ps[sh], wt, 1, sh)}
    if not end:
        ctail[lg] = turn(ps[lg], wt, 1, lg)

    def send(side):
        need("g", emit([ctail[side]], so[side], ps[side][:, tail], float(H * piece(rank, side))))
        g.remote_dma_fused([RemoteDMATransfer(dst_ids=ids(takers[side]), dma_engine_mask=bits(shared(rank)), remote_sem=S["ar%d" % rank],
                                              srcs=[so[side]], dsts=[T.ll[:, LW * rank:LW * rank + LW] for _ in takers[side]])], local_sem=S.ls)
        return len(shared(rank))

    gather(0, PLAN[-1][1], PLAN[-1][3])
    sent += send(sh)
    if end:
        first = [turn(T.cvb, wh, 0, sh), ctail[sh]]
        chead = turn(T.cvd, wh, 0, lg)
        ctail[lg] = turn(ps[lg], wt, 1, lg)
    else:
        chead = turn(T.cvb, wh, 0)
        sent += send(lg)

    stored = [0]

    def store(q, deps, rows, a, src):
        need(q, *deps)
        queue[q].dma_start(T.y[rows, a:a + src.shape[1]], src).then_inc(S.st, 16)
        stored[0] += 16

    if end:
        hw = LW // 2

        def split(x):
            src = ps[sh] if x else T.cvb
            return [emit([first[x]], T.ol[half(u), hw * x:hw * x + hw], src[half(u), LW * x + hw * u:LW * x + hw * u + hw]) for u in range(2)][-1]

        def unpack(x, listed, a, b, vc=None):
            o = W + 16 * hw * x
            t = jump([listed, z0, ("lo", 16 * len(own))], T.yo, o + 16 * a, T.se, H, T.ol, hw * x + a, hw * x + b, vc)
            for u in (range(2) if b == hw else []):
                store("y", t + [("ls", sent)], half(sh), W * x + 16 * hw * u, T.yo[half(u), o:o + 16 * hw])

        unpack(1, split(1), 0, hw, 16)
        listed = split(0)
    else:
        if spare == 1:
            emit([chead], T.ol[half(lg), head], T.cvb[half(lg), head], float(H * n))
            mine = emit([], T.ol[half(sh), head], ps[sh][half(sh), tail], float(H * slot(sh, m)))
        else:
            mine = emit([chead], T.ol[:, head], T.cvb[:, head], float(H * n))
        if spare == 0:
            emit([], T.ol[half(lg), tail], ps[lg][half(lg), tail], float(H * n))
            mine = emit([], T.ol[half(sh), tail], ps[sh][half(sh), tail], float(H * n))

    def arrived(src):
        return ("ar%d" % src, len(shared(src)))

    def short(k):
        if end or not lagged <= k < n:
            return []
        dst = T.ll[half(sh), LW * source[lg, k]:LW * source[lg, k] + LW]
        deps, j = [arrived(source[lg, k])], k - lagged
        if j < m:
            src = source[sh, j]
            return [emit(deps + [arrived(src)], dst, T.ll[half(sh), LW * src:LW * src + LW], float(H * (slot(sh, j) - j)))]
        return [emit(deps, dst, T.cvb[half(sh), head] if j == m else ps[sh][half(sh), tail], float(H * slot(sh, m)))]

    ready = [z0, ("lo", 16 * len(own))] + short(0)
    for k in range(n):
        src = source[lg, k]
        more = not end and lagged <= k + 1 < n
        ready = jump(ready + [("lw%d" % k, landed[k]), arrived(src)], T.sw, H * (k + 1) + NT, T.sw, H * (k + 1), T.ll, LW * src, LW * src + LW, VC if more else None)
        if not end and k >= lagged + m:
            store("y", ready, half(sh), W * (k - lagged - m), T.sw[half(sh), H * (k + 1) + NT:H * (k + 2)])
        ready = ready + short(k + 1)
        if end and k < 3:
            unpack(0, listed, hw // 3 * k, hw // 3 * (k + 1))
        if end and k == 3:
            emit([chead], T.ol[half(lg), tail], T.cvd[half(lg), head], float(H * n))
            mine = emit([ctail[lg]], T.ol[half(sh), tail], ps[lg][half(sh), tail], float(H * n))

    ready.append(mine)
    if end:
        t = jump(ready, T.yo, 0, T.sw, H * (n + 1), T.ol, LW, full)
        store("y", t, half(lg), 0, T.yo[half(lg), 0:W])
        store("s", t, half(lg), W, T.yo[half(sh), 0:W])
    elif spare:
        t = jump(ready, T.yo, 0, T.sw, H * (n + 1), T.ol, 0, LW)
        store("y", t, half(lg), 0, T.yo[half(lg), 0:W])
        store("y", t, half(sh), W, T.yo[half(sh), 0:W])
        t = jump(ready, T.yo, W, T.sw, H * (n + 1), T.so, LW * lg, LW * lg + LW)
        store("y", t, half(lg), W, T.yo[half(lg), W:P])
    else:
        for a, b in ((0, 16), (16, LW), (LW, full)):
            t = jump(ready, T.yo, 16 * a, T.sw, H * (n + 1), T.ol, a, b)
            store("y", t, slice(0, 128), 16 * a, T.yo[:, 16 * a:16 * b])
    g.wait_ge(S.ls, sent)
    need("y", ("st", stored[0]), *[("c" + q, cnt[q]) for q in cnt])
